import numpy as np
import ml_dtypes


def mxq(x, axis, fmt="e4m3"):
    dtype, down = {"e4m3": (ml_dtypes.float8_e4m3fn, 7), "e5m2": (ml_dtypes.float8_e5m2, 14)}[fmt]
    v = np.moveaxis(np.asarray(x, np.float32).astype(ml_dtypes.bfloat16).astype(np.float64), axis, -1)
    blocks = v.reshape(v.shape[:-1] + (-1, 32))
    amax = np.abs(blocks).max(-1, keepdims=True)
    byte = np.maximum(np.where(amax > 0, np.frexp(amax)[1] - 1 + 127, 0) - down, 1)
    scale = np.exp2(byte - 127.0)
    codes = (blocks / scale).astype(np.float32).astype(dtype).astype(np.float64)
    return np.moveaxis((codes * scale).reshape(v.shape), -1, axis)


WIDE = False


def mx_kscale(k):
    if not WIDE:
        return np.ones(k)
    levels = np.array([10, -10, 5, -5, 0])
    if k % 512:
        return np.exp2(np.random.permutation(np.resize(levels, k // 32))).repeat(32)
    a = np.empty((k // 512, 16))
    for p in range(k // 512):
        a[p, :8] = np.random.permutation(np.resize(levels, 8))
        for g in range(8):
            far = levels[np.abs(levels - a[p, g]) >= 10]
            a[p, g + 8] = far[np.random.randint(len(far))]
    return np.exp2(a.ravel()).repeat(32)


def f64(x):
    return np.asarray(x).astype(np.float64)


def striped(idx):
    return np.tile(idx.reshape(-1, 16).T, (8, 1)).astype(np.uint16)


def unstriped(offs):
    return offs[:16].T.reshape(-1).astype(np.int64)


E2M1 = np.array([0.0, 0.5, 1.0, 1.5, 2.0, 3.0, 4.0, 6.0, -0.0, -0.5, -1.0, -1.5, -2.0, -3.0, -4.0, -6.0])


def pack_weight(w, fmt):
    k, n = w.shape
    w = f64(np.asarray(w, np.float32).astype(ml_dtypes.bfloat16)).reshape(k // 32, 32, n)
    amax = np.abs(w).max(1)
    if fmt == "e4m3":
        byte = np.frexp(amax)[1] - 1 + 127 - 7
    else:
        mant, ex = np.frexp(amax / 6.0)
        byte = np.where(mant > 0.5, ex, ex - 1) + 127
    byte = np.clip(np.where(amax > 0, byte, 1), 1, 254)
    scaled = (w * np.exp2(127.0 - byte)[:, None, :]).reshape(k, n).astype(np.float32)
    by_word = np.ascontiguousarray(scaled.reshape(k // 512, 128, 4, n).transpose(0, 1, 3, 2))
    if fmt == "e4m3":
        words = by_word.astype(ml_dtypes.float8_e4m3fn).view(np.uint8)
    else:
        c = by_word.astype(ml_dtypes.float4_e2m1fn).view(np.uint8) & 0xF
        words = (c[..., 0::2] | (c[..., 1::2] << 4)).reshape(k // 512, 128, 2 * n)
    return np.ascontiguousarray(words), np.ascontiguousarray(byte.astype(np.uint8).reshape(k // 512, 16, n))


def unpack_weight(words, scales, fmt):
    g, _, n = scales.shape
    words = np.ascontiguousarray(words).reshape(g, 128, n, -1)
    if fmt == "e4m3":
        vals = words.view(ml_dtypes.float8_e4m3fn).astype(np.float64)
    else:
        nib = np.empty((g, 128, n, 4), np.uint8)
        nib[..., 0::2] = words & 0xF
        nib[..., 1::2] = words >> 4
        vals = E2M1[nib]
    vals = vals * np.repeat(np.exp2(scales.astype(np.float64) - 127.0), 8, axis=1)[..., None]
    return vals.transpose(0, 1, 3, 2).reshape(g * 512, n)


def pack_table(v):
    words, scales = pack_weight(v, "e4m3")
    return np.concatenate([words.reshape(words.shape[0], -1), scales.reshape(scales.shape[0], -1)], axis=1)


def unpack_table(tab):
    g, t = tab.shape[0], tab.shape[1] // 528
    return unpack_weight(tab[:, :512 * t].reshape(g, 128, t, 4), tab[:, 512 * t:].reshape(g, 16, t), "e4m3")


K, H, M, T, S = 512, 1536, 512, 2048, 1024


def setup_inputs():
    n = np.random.standard_normal
    s = mx_kscale(K)[:, None]
    u = mx_kscale(H)[:, None]
    w2 = 1.4 * n((H, M)) / np.sqrt(H) / u
    p_w8 = pack_weight(w2[:512], "e4m3")
    p_w4 = pack_weight(w2[512:], "e2m1")
    return {
        "tab": pack_table(n((K, T)) * s),
        "w1": (n((K, H)) / np.sqrt(K) / s * u.T).astype(np.float32),
        "w8_words": p_w8[0],
        "w8_scales": p_w8[1],
        "w4_words": p_w4[0],
        "w4_scales": p_w4[1],
        "offs": striped(np.random.permutation(T)[:S]),
    }


def reference(tab, w1, w8_words, w8_scales, w4_words, w4_scales, offs):
    tab_ = unpack_table(tab)[:, unstriped(offs)]
    w1_ = mxq(f64(w1), 0, "e4m3")
    w8_ = unpack_weight(w8_words, w8_scales, "e4m3")
    w4_ = unpack_weight(w4_words, w4_scales, "e2m1")
    h_ = mxq(np.maximum(w1_.T @ tab_, 0.0), 0, "e4m3")
    y = w8_.T @ h_[:512] + w4_.T @ h_[512:]
    return y

@@ -1,0 +1,245 @@
+from contextlib import ExitStack
+
+import concourse.mybir as mybir
+
+K, H, M, T, S = 512, 1536, 512, 2048, 1024
+FLOPS = 2 * S * (K * H + H * M)
+
+F32 = mybir.dt.float32
+BF16 = mybir.dt.bfloat16
+I32 = mybir.dt.int32
+U32 = mybir.dt.uint32
+U16 = mybir.dt.uint16
+U8 = mybir.dt.uint8
+E4M3 = mybir.dt.float8_e4m3fn_x4
+E2M1 = mybir.dt.float4_e2m1fn_x4
+RELU = mybir.ActivationFunctionType.Relu
+
+P = 128
+PACK = 4
+BLOCK = P * PACK
+N_BLOCKS = H // BLOCK
+HALF = 512
+CHUNK = 128
+CHUNKS = HALF // CHUNK
+M_TILES = M // P
+
+WARM_UP = 3
+PIECES = (2, 1, 1)
+LAY = {(0, 0): "SS", (0, 1): "SS", (1, 0): "VV", (2, 0): "VV"}
+RELU_ON = {(0, 0): "SSSS", (1, 0): "SSVS", (0, 1): "SSSS", (1, 1): "SSVS", (0, 2): "VSSS", (1, 2): "VSVS"}
+OUT_ON = {0: "SVSS", 1: "SVSV"}
+
+
+def tile_list_tabmlp_mix_none_kernel(tc, tab, w1, w8_words, w8_scales, w4_words, w4_scales, offs, out):
+    nc = tc.nc
+    with ExitStack() as ctx:
+        keep = ctx.enter_context(tc.tile_pool(name="keep", bufs=1))
+        psum_h = ctx.enter_context(tc.psum_pool(name="psum_h", bufs=5))
+        psum_o = ctx.enter_context(tc.psum_pool(name="psum_o", bufs=3))
+        store = ctx.enter_context(tc.tile_pool(name="store", bufs=8))
+
+        offsets = keep.tile([P, S // 16], U16, name="offsets")
+        nc.sync.dma_start(offsets[:], offs)
+
+        tab_scales = keep.tile([P, T // 4], I32, name="tab_scales", align_bytes=64)
+        nc.gpsimd.memset(tab_scales[:, 0 : T // 8], 0)
+        nc.vector.memset(tab_scales[:, T // 8 : T // 4], 0)
+        warm = keep.tile([P, 1], F32, name="warm")
+        warm_out = keep.tile([P, 1], F32, name="warm_out")
+        nc.vector.memset(warm[:], 0.0)
+        nc.scalar.activation(out=warm_out[:], in_=warm[:], func=RELU)
+
+        tab_words = keep.tile([P, T], I32, name="tab_words", align_bytes=64)
+        w_raw = {}
+        for b, pieces in enumerate(PIECES):
+            for i in range(pieces):
+                w_raw[b, i] = keep.tile([P, PACK, BLOCK // pieces], F32, name=f"w_raw{b}{i}")
+        w8 = keep.tile([P, M], U32, name="w8", align_bytes=64)
+        w4 = keep.tile([P, 2, 2 * M], U8, name="w4", align_bytes=64)
+        nc.gpsimd.memset(tab_words[:, 0:8], 0)
+        nc.gpsimd.memset(w_raw[0, 1][:, 0, 0:8], 0.0)
+        nc.gpsimd.memset(w_raw[1, 0][:, 0, 0:8], 0.0)
+        nc.gpsimd.memset(w_raw[2, 0][:, 0, 0:8], 0.0)
+        nc.gpsimd.memset(w8[:, 0:8].bitcast(I32), 0)
+        nc.gpsimd.memset(w4[:, 0, 0:32].bitcast(I32), 0)
+
+        w_scales = keep.tile([P, N_BLOCKS, M], U8, name="w_scales", align_bytes=64)
+        nc.gpsimd.memset(w_scales[:].rearrange("p a n -> p (a n)").bitcast(I32), 0)
+
+        w1_rows = w1.rearrange("(p j) r -> p j r", j=PACK)
+
+        def load_w1(b, i):
+            width = BLOCK // PIECES[b]
+            first = b * BLOCK + i * width
+            nc.sync.dma_start(w_raw[b, i][:], w1_rows[:, :, first : first + width])
+
+        load_w1(0, 0)
+        scale_rows = tab[0:1, 512 * T : 528 * T].rearrange("o (q t) -> (o q) t", q=16).bitcast(I32)
+        for q in range(4):
+            nc.sync.dma_start(tab_scales[32 * q : 32 * q + 4, :], scale_rows[4 * q : 4 * q + 4, :])
+        nc.sync.dma_start(tab_words[:], tab[0:1, 0 : 512 * T].rearrange("o (p x) -> (o p) x", p=P).bitcast(I32))
+        load_w1(0, 1)
+        load_w1(1, 0)
+        load_w1(2, 0)
+        for q in range(4):
+            rows = slice(4 * q, 4 * q + 4)
+            nc.sync.dma_start(
+                w_scales[32 * q : 32 * q + 4, 0, :].bitcast(I32),
+                w8_scales[0, rows, :].bitcast(I32),
+            )
+        nc.sync.dma_start(w8[:].bitcast(I32), w8_words.rearrange("a p n i -> (a p) (n i)").bitcast(I32))
+        for q in range(4):
+            rows = slice(4 * q, 4 * q + 4)
+            nc.sync.dma_start(
+                w_scales[32 * q : 32 * q + 4, 1:3, :].bitcast(I32),
+                w4_scales[:, rows, :].rearrange("a q n -> q a n").bitcast(I32),
+            )
+        nc.sync.dma_start(w4[:].bitcast(I32), w4_words.rearrange("a p x -> p a x").bitcast(I32))
+
+        x_codes = [keep.tile([P, HALF], U32, name=f"x_codes{i}", align_bytes=64) for i in range(2)]
+        x_scales = [keep.tile([P, HALF], U8, name=f"x_scales{i}", align_bytes=64) for i in range(2)]
+
+        def look_up(half, dst, window, pieces):
+            n = HALF // pieces
+            for i in range(pieces):
+                first = (half * HALF + i * n) // 16
+                part = offsets[:, first : first + n // 16]
+                nc.vector.tensor_copy(dst[half][:, i * n : (i + 1) * n], window.indirect(part))
+
+
+        def warm_up():
+            bank = psum_o.tile([P, HALF], F32, name="bank_o")
+            for i in range(WARM_UP):
+                nc.tensor.matmul_mx(
+                    out=bank[:],
+                    lhsT=x_codes[0][:, 0:P].bitcast(E4M3),
+                    lhsT_scale=x_scales[0][:, 0:P],
+                    rhs=x_codes[0][:].bitcast(E4M3),
+                    rhs_scale=x_scales[0][:],
+                    start=True,
+                    stop=True,
+                )
+
+        w_lay = [keep.tile([P, PACK * BLOCK], BF16, name=f"w_lay{b}", align_bytes=64) for b in range(N_BLOCKS)]
+        w1_codes = [keep.tile([P, BLOCK], U32, name=f"w1_codes{b}", align_bytes=64) for b in range(N_BLOCKS)]
+        w1_scales = [keep.tile([P, BLOCK], U8, name=f"w1_scales{b}", align_bytes=64) for b in range(N_BLOCKS)]
+
+        def lay_out_w1(b):
+            dst = w_lay[b][:].rearrange("p (t m j) -> p m j t", t=PACK, j=PACK)
+            for piece in range(PIECES[b]):
+                src = w_raw[b, piece][:].rearrange("p j (m t) -> p m j t", t=PACK)
+                engines = LAY[b, piece]
+                n = P // PIECES[b] // len(engines)
+                for i, engine in enumerate(engines):
+                    to = slice((piece * len(engines) + i) * n, (piece * len(engines) + i + 1) * n)
+                    if engine == "S":
+                        nc.scalar.copy(out=dst[:, to], in_=src[:, i * n : (i + 1) * n])
+                    else:
+                        nc.vector.tensor_copy(out=dst[:, to], in_=src[:, i * n : (i + 1) * n])
+
+        def quantize_w1(b):
+            for i in range(2):
+                cols = slice(i * BLOCK // 2, (i + 1) * BLOCK // 2)
+                nc.vector.quantize_mx(
+                    out=w1_codes[b][:, cols].bitcast(E4M3),
+                    scales=w1_scales[b][:, cols],
+                    in_=w_lay[b][:, i * 2 * BLOCK : (i + 1) * 2 * BLOCK],
+                )
+
+        h_lay = {}
+        h_codes = {}
+        h_scales = {}
+
+        def hidden(half, b):
+            lay = keep.tile([P, HALF, PACK], BF16, name=f"h_lay{half}{b}", align_bytes=64)
+            codes = keep.tile([P, HALF], U32, name=f"h_codes{half}{b}", align_bytes=64)
+            scales = keep.tile([P, HALF], U8, name=f"h_scales{half}{b}", align_bytes=64)
+            h_codes[half, b], h_scales[half, b] = codes, scales
+            for c in range(CHUNKS):
+                tokens = slice(c * CHUNK, (c + 1) * CHUNK)
+                bank = psum_h.tile([P, PACK, CHUNK], F32, name="bank_h")
+                for t in range(PACK):
+                    cols = slice(t * P, (t + 1) * P)
+                    nc.tensor.matmul_mx(
+                        out=bank[:, t, :],
+                        lhsT=w1_codes[b][:, cols].bitcast(E4M3),
+                        lhsT_scale=w1_scales[b][:, cols],
+                        rhs=x_codes[half][:, tokens].bitcast(E4M3),
+                        rhs_scale=x_scales[half][:, tokens],
+                        start=True,
+                        stop=True,
+                    )
+                by_token = bank[:].rearrange("p t n -> p n t")
+                if RELU_ON[half, b][c] == "S":
+                    nc.scalar.activation(out=lay[:, tokens, :], in_=by_token, func=RELU)
+                else:
+                    nc.vector.tensor_scalar_max(lay[:, tokens, :], by_token, 0.0)
+                if c % 2 == 1:
+                    pair = slice((c - 1) * CHUNK, (c + 1) * CHUNK)
+                    nc.vector.quantize_mx(
+                        out=codes[:, pair].bitcast(E4M3),
+                        scales=scales[:, pair],
+                        in_=lay[:, pair, :].rearrange("p n t -> p (n t)"),
+                    )
+
+        banks_o = {}
+
+        def project(half, b):
+            for n in range(M_TILES):
+                if b == 0:
+                    banks_o[half, n] = psum_o.tile([P, HALF], F32, name="bank_o")
+                if b == 0:
+                    lhsT = w8[:, n * P : (n + 1) * P].bitcast(E4M3)
+                else:
+                    lhsT = w4[:, b - 1, 2 * n * P : 2 * (n + 1) * P].bitcast(E2M1)
+                nc.tensor.matmul_mx(
+                    out=banks_o[half, n][:],
+                    lhsT=lhsT,
+                    lhsT_scale=w_scales[:, b, n * P : (n + 1) * P],
+                    rhs=h_codes[half, b][:].bitcast(E4M3),
+                    rhs_scale=h_scales[half, b][:],
+                    start=(b == 0),
+                    stop=(b == N_BLOCKS - 1),
+                )
+
+        def emit(half):
+            for n in range(M_TILES):
+                result = store.tile([P, HALF], F32, name="result")
+                if half == 1 and n == M_TILES - 1:
+                    mid = HALF // 2
+                    for cols in (slice(0, mid), slice(mid, HALF)):
+                        nc.vector.tensor_copy(out=result[:, cols], in_=banks_o[half, n][:, cols])
+                        nc.sync.dma_start(out[n * P : (n + 1) * P, HALF + cols.start : HALF + cols.stop], result[:, cols])
+                    continue
+                if OUT_ON[half][n] == "S":
+                    nc.scalar.copy(out=result[:], in_=banks_o[half, n][:])
+                else:
+                    nc.vector.tensor_copy(out=result[:], in_=banks_o[half, n][:])
+                nc.sync.dma_start(out[n * P : (n + 1) * P, half * HALF : (half + 1) * HALF], result[:])
+
+        look_up(0, x_scales, tab_scales[:].bitcast(U8), 1)
+        look_up(1, x_scales, tab_scales[:].bitcast(U8), 1)
+        look_up(0, x_codes, tab_words[:].bitcast(U32), 1)
+        warm_up()
+        look_up(1, x_codes, tab_words[:].bitcast(U32), 1)
+        lay_out_w1(0)
+        quantize_w1(0)
+        lay_out_w1(1)
+        quantize_w1(1)
+        lay_out_w1(2)
+        quantize_w1(2)
+        hidden(0, 0)
+        hidden(1, 0)
+        hidden(0, 1)
+        project(0, 0)
+        hidden(0, 2)
+        project(0, 1)
+        project(0, 2)
+        hidden(1, 1)
+        emit(0)
+        hidden(1, 2)
+        project(1, 0)
+        project(1, 1)
+        project(1, 2)
+        emit(1)

@@ -20,123 +20,83 @@ PACK = 4
 BLOCK = P * PACK
 N_BLOCKS = H // BLOCK
 HALF = 512
+QUARTER = 256
 CHUNK = 128
 CHUNKS = HALF // CHUNK
 M_TILES = M // P
-
-WARM_UP = 3
-PIECES = (2, 1, 1)
-LAY = {(0, 0): "SS", (0, 1): "SS", (1, 0): "VV", (2, 0): "VV"}
-RELU_ON = {(0, 0): "SSSS", (1, 0): "SSVS", (0, 1): "SSSS", (1, 1): "SSVS", (0, 2): "VSSS", (1, 2): "VSVS"}
-OUT_ON = {0: "SVSS", 1: "SVSV"}
+FIRST_COLS = 320
 
 
 def tile_list_tabmlp_mix_none_kernel(tc, tab, w1, w8_words, w8_scales, w4_words, w4_scales, offs, out):
     nc = tc.nc
     with ExitStack() as ctx:
         keep = ctx.enter_context(tc.tile_pool(name="keep", bufs=1))
-        psum_h = ctx.enter_context(tc.psum_pool(name="psum_h", bufs=5))
-        psum_o = ctx.enter_context(tc.psum_pool(name="psum_o", bufs=3))
+        psum = ctx.enter_context(tc.psum_pool(name="psum", bufs=1))
         store = ctx.enter_context(tc.tile_pool(name="store", bufs=8))
 
         offsets = keep.tile([P, S // 16], U16, name="offsets")
         nc.sync.dma_start(offsets[:], offs)
 
-        tab_scales = keep.tile([P, T // 4], I32, name="tab_scales", align_bytes=64)
-        nc.gpsimd.memset(tab_scales[:, 0 : T // 8], 0)
-        nc.vector.memset(tab_scales[:, T // 8 : T // 4], 0)
-        warm = keep.tile([P, 1], F32, name="warm")
-        warm_out = keep.tile([P, 1], F32, name="warm_out")
+        tab_scales = keep.tile([P, T // 4], I32, name="tab_scales", tag="table_scales", align_bytes=64)
+        nc.vector.memset(tab_scales[:, 0 : T // 8], 0)
+        nc.gpsimd.memset(tab_scales[:, T // 8 : T // 4], 0)
+        warm = keep.tile([P, 1], F32, name="warm", tag="table", align_bytes=64)
+        warm_out = keep.tile([P, 1], F32, name="warm_out", tag="stage1", align_bytes=64)
         nc.vector.memset(warm[:], 0.0)
         nc.scalar.activation(out=warm_out[:], in_=warm[:], func=RELU)
 
-        tab_words = keep.tile([P, T], I32, name="tab_words", align_bytes=64)
-        w_raw = {}
-        for b, pieces in enumerate(PIECES):
-            for i in range(pieces):
-                w_raw[b, i] = keep.tile([P, PACK, BLOCK // pieces], F32, name=f"w_raw{b}{i}")
-        w8 = keep.tile([P, M], U32, name="w8", align_bytes=64)
-        w4 = keep.tile([P, 2, 2 * M], U8, name="w4", align_bytes=64)
-        nc.gpsimd.memset(tab_words[:, 0:8], 0)
-        nc.gpsimd.memset(w_raw[0, 1][:, 0, 0:8], 0.0)
-        nc.gpsimd.memset(w_raw[1, 0][:, 0, 0:8], 0.0)
-        nc.gpsimd.memset(w_raw[2, 0][:, 0, 0:8], 0.0)
-        nc.gpsimd.memset(w8[:, 0:8].bitcast(I32), 0)
-        nc.gpsimd.memset(w4[:, 0, 0:32].bitcast(I32), 0)
-
+        tab_words = keep.tile([P, T], I32, name="tab_words", tag="table", align_bytes=64)
         w_scales = keep.tile([P, N_BLOCKS, M], U8, name="w_scales", align_bytes=64)
         nc.gpsimd.memset(w_scales[:].rearrange("p a n -> p (a n)").bitcast(I32), 0)
 
         w1_rows = w1.rearrange("(p j) r -> p j r", j=PACK)
 
-        def load_w1(b, i):
-            width = BLOCK // PIECES[b]
-            first = b * BLOCK + i * width
-            nc.sync.dma_start(w_raw[b, i][:], w1_rows[:, :, first : first + width])
+        w_raw = {}
 
-        load_w1(0, 0)
+        def load_w1(b, first, last, tag):
+            w_raw[b, first] = keep.tile([P, PACK, last - first], F32, name=f"w_raw{b}_{first}", tag=tag, align_bytes=64)
+            nc.sync.dma_start(w_raw[b, first][:], w1_rows[:, :, b * BLOCK + first : b * BLOCK + last])
+
+        def load_w_scales(planes, source):
+            for q in range(4):
+                nc.gpsimd.dma_start(
+                    w_scales[32 * q : 32 * q + 4, planes, :].bitcast(I32),
+                    source[:, 4 * q : 4 * q + 4, :].rearrange("a q n -> q a n").bitcast(I32),
+                )
+
+        load_w1(0, 0, FIRST_COLS, "stage0")
         scale_rows = tab[0:1, 512 * T : 528 * T].rearrange("o (q t) -> (o q) t", q=16).bitcast(I32)
         for q in range(4):
             nc.sync.dma_start(tab_scales[32 * q : 32 * q + 4, :], scale_rows[4 * q : 4 * q + 4, :])
+        load_w1(0, FIRST_COLS, BLOCK, "stage1")
         nc.sync.dma_start(tab_words[:], tab[0:1, 0 : 512 * T].rearrange("o (p x) -> (o p) x", p=P).bitcast(I32))
-        load_w1(0, 1)
-        load_w1(1, 0)
-        load_w1(2, 0)
-        for q in range(4):
-            rows = slice(4 * q, 4 * q + 4)
-            nc.sync.dma_start(
-                w_scales[32 * q : 32 * q + 4, 0, :].bitcast(I32),
-                w8_scales[0, rows, :].bitcast(I32),
-            )
-        nc.sync.dma_start(w8[:].bitcast(I32), w8_words.rearrange("a p n i -> (a p) (n i)").bitcast(I32))
-        for q in range(4):
-            rows = slice(4 * q, 4 * q + 4)
-            nc.sync.dma_start(
-                w_scales[32 * q : 32 * q + 4, 1:3, :].bitcast(I32),
-                w4_scales[:, rows, :].rearrange("a q n -> q a n").bitcast(I32),
-            )
-        nc.sync.dma_start(w4[:].bitcast(I32), w4_words.rearrange("a p x -> p a x").bitcast(I32))
 
-        x_codes = [keep.tile([P, HALF], U32, name=f"x_codes{i}", align_bytes=64) for i in range(2)]
-        x_scales = [keep.tile([P, HALF], U8, name=f"x_scales{i}", align_bytes=64) for i in range(2)]
+        x_codes = [keep.tile([P, QUARTER], U32, name=f"x_codes{i}", align_bytes=64) for i in range(4)]
+        x_scales = [keep.tile([P, QUARTER], U8, name=f"x_scales{i}", align_bytes=64) for i in range(4)]
 
-        def look_up(half, dst, window, pieces):
-            n = HALF // pieces
-            for i in range(pieces):
-                first = (half * HALF + i * n) // 16
-                part = offsets[:, first : first + n // 16]
-                nc.vector.tensor_copy(dst[half][:, i * n : (i + 1) * n], window.indirect(part))
+        def look_up(dst, window, quarter):
+            part = offsets[:, quarter * QUARTER // 16 : (quarter + 1) * QUARTER // 16]
+            nc.vector.tensor_copy(dst[quarter][:], window.indirect(part))
 
+        def look_up_scales(quarter):
+            look_up(x_scales, tab_scales[:].bitcast(U8), quarter)
 
-        def warm_up():
-            bank = psum_o.tile([P, HALF], F32, name="bank_o")
-            for i in range(WARM_UP):
-                nc.tensor.matmul_mx(
-                    out=bank[:],
-                    lhsT=x_codes[0][:, 0:P].bitcast(E4M3),
-                    lhsT_scale=x_scales[0][:, 0:P],
-                    rhs=x_codes[0][:].bitcast(E4M3),
-                    rhs_scale=x_scales[0][:],
-                    start=True,
-                    stop=True,
-                )
+        def look_up_words(quarter):
+            look_up(x_codes, tab_words[:].bitcast(U32), quarter)
 
-        w_lay = [keep.tile([P, PACK * BLOCK], BF16, name=f"w_lay{b}", align_bytes=64) for b in range(N_BLOCKS)]
+        w_lay = [
+            keep.tile([P, PACK * BLOCK], BF16, name=f"w_lay{b}", tag=f"w_lay{b}", align_bytes=64) for b in range(N_BLOCKS)
+        ]
         w1_codes = [keep.tile([P, BLOCK], U32, name=f"w1_codes{b}", align_bytes=64) for b in range(N_BLOCKS)]
         w1_scales = [keep.tile([P, BLOCK], U8, name=f"w1_scales{b}", align_bytes=64) for b in range(N_BLOCKS)]
 
-        def lay_out_w1(b):
+        def lay_out_w1(b, loaded_from, first, last, copy):
             dst = w_lay[b][:].rearrange("p (t m j) -> p m j t", t=PACK, j=PACK)
-            for piece in range(PIECES[b]):
-                src = w_raw[b, piece][:].rearrange("p j (m t) -> p m j t", t=PACK)
-                engines = LAY[b, piece]
-                n = P // PIECES[b] // len(engines)
-                for i, engine in enumerate(engines):
-                    to = slice((piece * len(engines) + i) * n, (piece * len(engines) + i + 1) * n)
-                    if engine == "S":
-                        nc.scalar.copy(out=dst[:, to], in_=src[:, i * n : (i + 1) * n])
-                    else:
-                        nc.vector.tensor_copy(out=dst[:, to], in_=src[:, i * n : (i + 1) * n])
+            src = w_raw[b, loaded_from][:].rearrange("p j (m t) -> p m j t", t=PACK)
+            copy(
+                out=dst[:, first // PACK : last // PACK],
+                in_=src[:, (first - loaded_from) // PACK : (last - loaded_from) // PACK],
+            )
 
         def quantize_w1(b):
             for i in range(2):
@@ -147,34 +107,35 @@ def tile_list_tabmlp_mix_none_kernel(tc, tab, w1, w8_words, w8_scales, w4_words,
                     in_=w_lay[b][:, i * 2 * BLOCK : (i + 1) * 2 * BLOCK],
                 )
 
-        h_lay = {}
         h_codes = {}
         h_scales = {}
 
-        def hidden(half, b):
+        def hidden(half, b, first_bank, vector_chunks):
             lay = keep.tile([P, HALF, PACK], BF16, name=f"h_lay{half}{b}", align_bytes=64)
             codes = keep.tile([P, HALF], U32, name=f"h_codes{half}{b}", align_bytes=64)
             scales = keep.tile([P, HALF], U8, name=f"h_scales{half}{b}", align_bytes=64)
             h_codes[half, b], h_scales[half, b] = codes, scales
             for c in range(CHUNKS):
                 tokens = slice(c * CHUNK, (c + 1) * CHUNK)
-                bank = psum_h.tile([P, PACK, CHUNK], F32, name="bank_h")
+                quarter = 2 * half + c // 2
+                picked = slice(c % 2 * CHUNK, (c % 2 + 1) * CHUNK)
+                bank = psum.tile([P, PACK, CHUNK], F32, name=f"bank{first_bank + c}")
                 for t in range(PACK):
                     cols = slice(t * P, (t + 1) * P)
                     nc.tensor.matmul_mx(
                         out=bank[:, t, :],
                         lhsT=w1_codes[b][:, cols].bitcast(E4M3),
                         lhsT_scale=w1_scales[b][:, cols],
-                        rhs=x_codes[half][:, tokens].bitcast(E4M3),
-                        rhs_scale=x_scales[half][:, tokens],
+                        rhs=x_codes[quarter][:, picked].bitcast(E4M3),
+                        rhs_scale=x_scales[quarter][:, picked],
                         start=True,
                         stop=True,
                     )
                 by_token = bank[:].rearrange("p t n -> p n t")
-                if RELU_ON[half, b][c] == "S":
-                    nc.scalar.activation(out=lay[:, tokens, :], in_=by_token, func=RELU)
-                else:
+                if c in vector_chunks:
                     nc.vector.tensor_scalar_max(lay[:, tokens, :], by_token, 0.0)
+                else:
+                    nc.scalar.activation(out=lay[:, tokens, :], in_=by_token, func=RELU)
                 if c % 2 == 1:
                     pair = slice((c - 1) * CHUNK, (c + 1) * CHUNK)
                     nc.vector.quantize_mx(
@@ -185,61 +146,65 @@ def tile_list_tabmlp_mix_none_kernel(tc, tab, w1, w8_words, w8_scales, w4_words,
 
         banks_o = {}
 
-        def project(half, b):
-            for n in range(M_TILES):
-                if b == 0:
-                    banks_o[half, n] = psum_o.tile([P, HALF], F32, name="bank_o")
-                if b == 0:
-                    lhsT = w8[:, n * P : (n + 1) * P].bitcast(E4M3)
-                else:
-                    lhsT = w4[:, b - 1, 2 * n * P : 2 * (n + 1) * P].bitcast(E2M1)
-                nc.tensor.matmul_mx(
-                    out=banks_o[half, n][:],
-                    lhsT=lhsT,
-                    lhsT_scale=w_scales[:, b, n * P : (n + 1) * P],
-                    rhs=h_codes[half, b][:].bitcast(E4M3),
-                    rhs_scale=h_scales[half, b][:],
-                    start=(b == 0),
-                    stop=(b == N_BLOCKS - 1),
-                )
+        def project(half, n, b, first_bank):
+            if b == 0:
+                banks_o[half, n] = psum.tile([P, HALF], F32, name=f"bank{first_bank + n}")
+                lhsT = w8[:, n * P : (n + 1) * P].bitcast(E4M3)
+            else:
+                lhsT = w4[:, b - 1, 2 * n * P : 2 * (n + 1) * P].bitcast(E2M1)
+            nc.tensor.matmul_mx(
+                out=banks_o[half, n][:],
+                lhsT=lhsT,
+                lhsT_scale=w_scales[:, b, n * P : (n + 1) * P],
+                rhs=h_codes[half, b][:].bitcast(E4M3),
+                rhs_scale=h_scales[half, b][:],
+                start=(b == 0),
+                stop=(b == N_BLOCKS - 1),
+            )
 
-        def emit(half):
-            for n in range(M_TILES):
-                result = store.tile([P, HALF], F32, name="result")
-                if half == 1 and n == M_TILES - 1:
-                    mid = HALF // 2
-                    for cols in (slice(0, mid), slice(mid, HALF)):
-                        nc.vector.tensor_copy(out=result[:, cols], in_=banks_o[half, n][:, cols])
-                        nc.sync.dma_start(out[n * P : (n + 1) * P, HALF + cols.start : HALF + cols.stop], result[:, cols])
-                    continue
-                if OUT_ON[half][n] == "S":
-                    nc.scalar.copy(out=result[:], in_=banks_o[half, n][:])
-                else:
-                    nc.vector.tensor_copy(out=result[:], in_=banks_o[half, n][:])
-                nc.sync.dma_start(out[n * P : (n + 1) * P, half * HALF : (half + 1) * HALF], result[:])
+        def emit(half, n):
+            result = store.tile([P, HALF], F32, name="result")
+            if n % 2 == 0:
+                nc.scalar.copy(out=result[:], in_=banks_o[half, n][:])
+            else:
+                nc.vector.tensor_copy(out=result[:], in_=banks_o[half, n][:])
+            nc.sync.dma_start(out[n * P : (n + 1) * P, half * HALF : (half + 1) * HALF], result[:])
 
-        look_up(0, x_scales, tab_scales[:].bitcast(U8), 1)
-        look_up(1, x_scales, tab_scales[:].bitcast(U8), 1)
-        look_up(0, x_codes, tab_words[:].bitcast(U32), 1)
-        warm_up()
-        look_up(1, x_codes, tab_words[:].bitcast(U32), 1)
-        lay_out_w1(0)
+        load_w_scales(slice(0, 1), w8_scales)
+        load_w_scales(slice(1, 3), w4_scales)
+        lay_out_w1(0, 0, 0, FIRST_COLS, nc.scalar.copy)
+        load_w1(1, 0, BLOCK, "stage0")
+        lay_out_w1(0, FIRST_COLS, FIRST_COLS, BLOCK, nc.scalar.copy)
+        w8 = keep.tile([P, M], U32, name="w8", tag="stage1", align_bytes=64)
+        nc.sync.dma_start(w8[:].bitcast(I32), w8_words.rearrange("a p n i -> (a p) (n i)").bitcast(I32))
+        for quarter in range(4):
+            look_up_scales(quarter)
         quantize_w1(0)
-        lay_out_w1(1)
+        load_w1(2, 0, BLOCK, "w_lay0")
+        for quarter in range(4):
+            look_up_words(quarter)
+        w4 = keep.tile([P, 2, 2 * M], U8, name="w4", tag="table", align_bytes=64)
+        nc.sync.dma_start(w4[:].bitcast(I32), w4_words.rearrange("a p x -> p a x").bitcast(I32))
+        lay_out_w1(1, 0, 0, BLOCK // 2, nc.vector.tensor_copy)
+        lay_out_w1(1, 0, BLOCK // 2, BLOCK, nc.vector.tensor_copy)
         quantize_w1(1)
-        lay_out_w1(2)
+        hidden(0, 0, 0, ())
+        hidden(1, 0, 4, ())
+        lay_out_w1(2, 0, 0, BLOCK // 2, nc.vector.tensor_copy)
+        lay_out_w1(2, 0, BLOCK // 2, BLOCK, nc.vector.tensor_copy)
         quantize_w1(2)
-        hidden(0, 0)
-        hidden(1, 0)
-        hidden(0, 1)
-        project(0, 0)
-        hidden(0, 2)
-        project(0, 1)
-        project(0, 2)
-        hidden(1, 1)
-        emit(0)
-        hidden(1, 2)
-        project(1, 0)
-        project(1, 1)
-        project(1, 2)
-        emit(1)
+        hidden(0, 1, 4, ())
+        for n in range(M_TILES):
+            project(0, n, 0, 0)
+        hidden(1, 1, 4, (2,))
+        hidden(0, 2, 4, (0, 2))
+        for n in range(M_TILES):
+            project(0, n, 1, 0)
+        hidden(1, 2, 4, (0, 2))
+        for n in range(M_TILES):
+            project(0, n, 2, 0)
+            emit(0, n)
+        for n in range(M_TILES):
+            for b in range(N_BLOCKS):
+                project(1, n, b, 4)
+            emit(1, n)

@@ -24,7 +24,10 @@ QUARTER = 256
 CHUNK = 128
 CHUNKS = HALF // CHUNK
 M_TILES = M // P
-FIRST_COLS = 320
+W8_ROW = 4
+TABLE_ROW = 8
+FIRST_COLS = 256
+SECOND_COLS = 256
 
 
 def tile_list_tabmlp_mix_none_kernel(tc, tab, w1, w8_words, w8_scales, w4_words, w4_scales, offs, out):
@@ -46,8 +49,6 @@ def tile_list_tabmlp_mix_none_kernel(tc, tab, w1, w8_words, w8_scales, w4_words,
         nc.scalar.activation(out=warm_out[:], in_=warm[:], func=RELU)
 
         tab_words = keep.tile([P, T], I32, name="tab_words", tag="table", align_bytes=64)
-        w_scales = keep.tile([P, N_BLOCKS, M], U8, name="w_scales", align_bytes=64)
-        nc.gpsimd.memset(w_scales[:].rearrange("p a n -> p (a n)").bitcast(I32), 0)
 
         w1_rows = w1.rearrange("(p j) r -> p j r", j=PACK)
 
@@ -57,17 +58,17 @@ def tile_list_tabmlp_mix_none_kernel(tc, tab, w1, w8_words, w8_scales, w4_words,
             w_raw[b, first] = keep.tile([P, PACK, last - first], F32, name=f"w_raw{b}_{first}", tag=tag, align_bytes=64)
             nc.sync.dma_start(w_raw[b, first][:], w1_rows[:, :, b * BLOCK + first : b * BLOCK + last])
 
-        def load_w_scales(planes, source):
+        def load_w_scales(queue, planes, first_row, source):
             for q in range(4):
-                nc.gpsimd.dma_start(
-                    w_scales[32 * q : 32 * q + 4, planes, :].bitcast(I32),
+                queue.dma_start(
+                    planes[32 * q + first_row : 32 * q + first_row + 4],
                     source[:, 4 * q : 4 * q + 4, :].rearrange("a q n -> q a n").bitcast(I32),
                 )
 
         load_w1(0, 0, FIRST_COLS, "stage0")
         scale_rows = tab[0:1, 512 * T : 528 * T].rearrange("o (q t) -> (o q) t", q=16).bitcast(I32)
         for q in range(4):
-            nc.sync.dma_start(tab_scales[32 * q : 32 * q + 4, :], scale_rows[4 * q : 4 * q + 4, :])
+            nc.sync.dma_start(tab_scales[32 * q + TABLE_ROW : 32 * q + TABLE_ROW + 4, :], scale_rows[4 * q : 4 * q + 4, :])
         load_w1(0, FIRST_COLS, BLOCK, "stage1")
         nc.sync.dma_start(tab_words[:], tab[0:1, 0 : 512 * T].rearrange("o (p x) -> (o p) x", p=P).bitcast(I32))
 
@@ -111,8 +112,11 @@ def tile_list_tabmlp_mix_none_kernel(tc, tab, w1, w8_words, w8_scales, w4_words,
         h_scales = {}
 
         def hidden(half, b, first_bank, vector_chunks):
-            lay = keep.tile([P, HALF, PACK], BF16, name=f"h_lay{half}{b}", align_bytes=64)
-            codes = keep.tile([P, HALF], U32, name=f"h_codes{half}{b}", align_bytes=64)
+            first = half == 0 and b == 0
+            lay_tag = ("stage0", "table_scales")[half] if b == 0 else f"h_lay{half}{b}"
+            codes_tag = "w_lay1" if first else f"h_codes{half}{b}"
+            lay = keep.tile([P, HALF, PACK], BF16, name=f"h_lay{half}{b}", tag=lay_tag, align_bytes=64)
+            codes = keep.tile([P, HALF], U32, name=f"h_codes{half}{b}", tag=codes_tag, align_bytes=64)
             scales = keep.tile([P, HALF], U8, name=f"h_scales{half}{b}", align_bytes=64)
             h_codes[half, b], h_scales[half, b] = codes, scales
             for c in range(CHUNKS):
@@ -127,7 +131,7 @@ def tile_list_tabmlp_mix_none_kernel(tc, tab, w1, w8_words, w8_scales, w4_words,
                         lhsT=w1_codes[b][:, cols].bitcast(E4M3),
                         lhsT_scale=w1_scales[b][:, cols],
                         rhs=x_codes[quarter][:, picked].bitcast(E4M3),
-                        rhs_scale=x_scales[quarter][:, picked],
+                        rhs_scale=x_scales[quarter][TABLE_ROW:, picked],
                         start=True,
                         stop=True,
                     )
@@ -136,8 +140,9 @@ def tile_list_tabmlp_mix_none_kernel(tc, tab, w1, w8_words, w8_scales, w4_words,
                     nc.vector.tensor_scalar_max(lay[:, tokens, :], by_token, 0.0)
                 else:
                     nc.scalar.activation(out=lay[:, tokens, :], in_=by_token, func=RELU)
-                if c % 2 == 1:
-                    pair = slice((c - 1) * CHUNK, (c + 1) * CHUNK)
+                together = CHUNKS if half == 1 and b < N_BLOCKS - 1 else 2
+                if (c + 1) % together == 0:
+                    pair = slice((c + 1 - together) * CHUNK, (c + 1) * CHUNK)
                     nc.vector.quantize_mx(
                         out=codes[:, pair].bitcast(E4M3),
                         scales=scales[:, pair],
@@ -146,16 +151,21 @@ def tile_list_tabmlp_mix_none_kernel(tc, tab, w1, w8_words, w8_scales, w4_words,
 
         banks_o = {}
 
+        def second_weights(n, b):
+            planes = slice(n * P // 4, (n + 1) * P // 4)
+            if b == 0:
+                return w8[:, n * P : (n + 1) * P].bitcast(E4M3), w8_plane[W8_ROW:, 0, planes].bitcast(U8)
+            words = w4[:, b - 1, n * P // 2 : (n + 1) * P // 2]
+            return words.bitcast(U8).bitcast(E2M1), w4_planes[:, b - 1, planes].bitcast(U8)
+
         def project(half, n, b, first_bank):
             if b == 0:
                 banks_o[half, n] = psum.tile([P, HALF], F32, name=f"bank{first_bank + n}")
-                lhsT = w8[:, n * P : (n + 1) * P].bitcast(E4M3)
-            else:
-                lhsT = w4[:, b - 1, 2 * n * P : 2 * (n + 1) * P].bitcast(E2M1)
+            lhsT, lhsT_scale = second_weights(n, b)
             nc.tensor.matmul_mx(
                 out=banks_o[half, n][:],
                 lhsT=lhsT,
-                lhsT_scale=w_scales[:, b, n * P : (n + 1) * P],
+                lhsT_scale=lhsT_scale,
                 rhs=h_codes[half, b][:].bitcast(E4M3),
                 rhs_scale=h_scales[half, b][:],
                 start=(b == 0),
@@ -164,47 +174,75 @@ def tile_list_tabmlp_mix_none_kernel(tc, tab, w1, w8_words, w8_scales, w4_words,
 
         def emit(half, n):
             result = store.tile([P, HALF], F32, name="result")
-            if n % 2 == 0:
+            if n % 2 == 1:
                 nc.scalar.copy(out=result[:], in_=banks_o[half, n][:])
             else:
                 nc.vector.tensor_copy(out=result[:], in_=banks_o[half, n][:])
             nc.sync.dma_start(out[n * P : (n + 1) * P, half * HALF : (half + 1) * HALF], result[:])
 
-        load_w_scales(slice(0, 1), w8_scales)
-        load_w_scales(slice(1, 3), w4_scales)
+        def last_tile(quarter, bank_number, copy):
+            n = M_TILES - 1
+            bank = psum.tile([P, QUARTER], F32, name=f"bank{bank_number}")
+            first = quarter * QUARTER
+            passes = [(0, 0, QUARTER)] + [(b, c, c + CHUNK) for b in (1, 2) for c in (0, CHUNK)]
+            for i, (b, lo, hi) in enumerate(passes):
+                lhsT, lhsT_scale = second_weights(n, b)
+                nc.tensor.matmul_mx(
+                    out=bank[:, lo:hi],
+                    lhsT=lhsT,
+                    lhsT_scale=lhsT_scale,
+                    rhs=h_codes[1, b][:, first + lo : first + hi].bitcast(E4M3),
+                    rhs_scale=h_scales[1, b][:, first + lo : first + hi],
+                    start=(i == 0),
+                    stop=(i == len(passes) - 1),
+                )
+            result = store.tile([P, QUARTER], F32, name="result")
+            copy(out=result[:], in_=bank[:])
+            nc.sync.dma_start(out[n * P : (n + 1) * P, HALF + first : HALF + first + QUARTER], result[:])
+
+        w4_planes = keep.tile([P, 2, M // 4], I32, name="w4_planes", align_bytes=64)
+        nc.gpsimd.memset(w4_planes[:], 0)
+        load_w_scales(nc.gpsimd, w4_planes, 0, w4_scales)
         lay_out_w1(0, 0, 0, FIRST_COLS, nc.scalar.copy)
-        load_w1(1, 0, BLOCK, "stage0")
+        load_w1(1, 0, SECOND_COLS, "stage0")
         lay_out_w1(0, FIRST_COLS, FIRST_COLS, BLOCK, nc.scalar.copy)
-        w8 = keep.tile([P, M], U32, name="w8", tag="stage1", align_bytes=64)
-        nc.sync.dma_start(w8[:].bitcast(I32), w8_words.rearrange("a p n i -> (a p) (n i)").bitcast(I32))
         for quarter in range(4):
             look_up_scales(quarter)
+        load_w1(1, SECOND_COLS, BLOCK, "table_scales")
+        load_w1(2, 0, BLOCK, "stage1")
         quantize_w1(0)
-        load_w1(2, 0, BLOCK, "w_lay0")
+        w2 = keep.tile([P, 2 * M + M // 4], I32, name="w2", tag="w_lay0", align_bytes=64)
+        w8 = w2[:, 0:M]
+        w4 = w2[:, M : 2 * M].rearrange("p (a x) -> p a x", a=2)
+        w8_plane = w2[:, 2 * M :].rearrange("p (a x) -> p a x", a=1)
+        nc.gpsimd.memset(w2[:, 2 * M :], 0)
+        nc.sync.dma_start(w8, w8_words.rearrange("a p n i -> (a p) (n i)").bitcast(I32))
+        load_w_scales(nc.scalar, w8_plane, W8_ROW, w8_scales)
+        nc.sync.dma_start(w4, w4_words.rearrange("a p x -> p a x").bitcast(I32))
         for quarter in range(4):
             look_up_words(quarter)
-        w4 = keep.tile([P, 2, 2 * M], U8, name="w4", tag="table", align_bytes=64)
-        nc.sync.dma_start(w4[:].bitcast(I32), w4_words.rearrange("a p x -> p a x").bitcast(I32))
-        lay_out_w1(1, 0, 0, BLOCK // 2, nc.vector.tensor_copy)
-        lay_out_w1(1, 0, BLOCK // 2, BLOCK, nc.vector.tensor_copy)
+        lay_out_w1(1, 0, 0, SECOND_COLS, nc.scalar.copy)
+        lay_out_w1(1, SECOND_COLS, SECOND_COLS, BLOCK, nc.vector.tensor_copy)
         quantize_w1(1)
-        hidden(0, 0, 0, ())
+        hidden(0, 0, 4, ())
         hidden(1, 0, 4, ())
         lay_out_w1(2, 0, 0, BLOCK // 2, nc.vector.tensor_copy)
         lay_out_w1(2, 0, BLOCK // 2, BLOCK, nc.vector.tensor_copy)
         quantize_w1(2)
-        hidden(0, 1, 4, ())
+        hidden(0, 1, 4, (2,))
+        hidden(1, 1, 4, (2,))
         for n in range(M_TILES):
             project(0, n, 0, 0)
-        hidden(1, 1, 4, (2,))
-        hidden(0, 2, 4, (0, 2))
+        hidden(0, 2, 4, (2,))
+        hidden(1, 2, 4, (0, 2))
         for n in range(M_TILES):
             project(0, n, 1, 0)
-        hidden(1, 2, 4, (0, 2))
         for n in range(M_TILES):
             project(0, n, 2, 0)
             emit(0, n)
-        for n in range(M_TILES):
+        for n in range(M_TILES - 1):
             for b in range(N_BLOCKS):
                 project(1, n, b, 4)
             emit(1, n)
+        last_tile(0, 7, nc.scalar.copy)
+        last_tile(1, 0, nc.vector.tensor_copy)

@@ -24,10 +24,11 @@ QUARTER = 256
 CHUNK = 128
 CHUNKS = HALF // CHUNK
 M_TILES = M // P
+RING_FIRST, RING = 4, 4
+VECTOR_FROM, VECTOR_EVERY = 6, 4
 W8_ROW = 4
 TABLE_ROW = 8
 FIRST_COLS = 256
-SECOND_COLS = 256
 
 
 def tile_list_tabmlp_mix_none_kernel(tc, tab, w1, w8_words, w8_scales, w4_words, w4_scales, offs, out):
@@ -40,7 +41,7 @@ def tile_list_tabmlp_mix_none_kernel(tc, tab, w1, w8_words, w8_scales, w4_words,
         offsets = keep.tile([P, S // 16], U16, name="offsets")
         nc.sync.dma_start(offsets[:], offs)
 
-        tab_scales = keep.tile([P, T // 4], I32, name="tab_scales", tag="table_scales", align_bytes=64)
+        tab_scales = keep.tile([P, T // 4], I32, name="tab_scales", align_bytes=64)
         nc.vector.memset(tab_scales[:, 0 : T // 8], 0)
         nc.gpsimd.memset(tab_scales[:, T // 8 : T // 4], 0)
         warm = keep.tile([P, 1], F32, name="warm", tag="table", align_bytes=64)
@@ -111,19 +112,23 @@ def tile_list_tabmlp_mix_none_kernel(tc, tab, w1, w8_words, w8_scales, w4_words,
         h_codes = {}
         h_scales = {}
 
-        def hidden(half, b, first_bank, vector_chunks):
-            first = half == 0 and b == 0
-            lay_tag = ("stage0", "table_scales")[half] if b == 0 else f"h_lay{half}{b}"
-            codes_tag = "w_lay1" if first else f"h_codes{half}{b}"
-            lay = keep.tile([P, HALF, PACK], BF16, name=f"h_lay{half}{b}", tag=lay_tag, align_bytes=64)
-            codes = keep.tile([P, HALF], U32, name=f"h_codes{half}{b}", tag=codes_tag, align_bytes=64)
-            scales = keep.tile([P, HALF], U8, name=f"h_scales{half}{b}", align_bytes=64)
-            h_codes[half, b], h_scales[half, b] = codes, scales
-            for c in range(CHUNKS):
+        h_lay = {}
+        done = []
+
+        def hidden(half, b, chunks):
+            if (half, b) not in h_lay:
+                lay_tag = "stage0" if half == 1 and b == 0 else f"h_lay{half}{b}"
+                codes_tag = "w_lay1" if half == 0 and b == 0 else f"h_codes{half}{b}"
+                h_lay[half, b] = keep.tile([P, HALF, PACK], BF16, name=f"h_lay{half}{b}", tag=lay_tag, align_bytes=64)
+                h_codes[half, b] = keep.tile([P, HALF], U32, name=f"h_codes{half}{b}", tag=codes_tag, align_bytes=64)
+                h_scales[half, b] = keep.tile([P, HALF], U8, name=f"h_scales{half}{b}", align_bytes=64)
+            for c in chunks:
+                step = len(done)
+                done.append((half, b, c))
                 tokens = slice(c * CHUNK, (c + 1) * CHUNK)
                 quarter = 2 * half + c // 2
                 picked = slice(c % 2 * CHUNK, (c % 2 + 1) * CHUNK)
-                bank = psum.tile([P, PACK, CHUNK], F32, name=f"bank{first_bank + c}")
+                bank = psum.tile([P, PACK, CHUNK], F32, name=f"bank{RING_FIRST + step % RING}")
                 for t in range(PACK):
                     cols = slice(t * P, (t + 1) * P)
                     nc.tensor.matmul_mx(
@@ -136,18 +141,20 @@ def tile_list_tabmlp_mix_none_kernel(tc, tab, w1, w8_words, w8_scales, w4_words,
                         stop=True,
                     )
                 by_token = bank[:].rearrange("p t n -> p n t")
-                if c in vector_chunks:
-                    nc.vector.tensor_scalar_max(lay[:, tokens, :], by_token, 0.0)
+                if step >= VECTOR_FROM and (step - VECTOR_FROM) % VECTOR_EVERY == 0:
+                    nc.vector.tensor_scalar_max(h_lay[half, b][:, tokens, :], by_token, 0.0)
                 else:
-                    nc.scalar.activation(out=lay[:, tokens, :], in_=by_token, func=RELU)
-                together = CHUNKS if half == 1 and b < N_BLOCKS - 1 else 2
-                if (c + 1) % together == 0:
-                    pair = slice((c + 1 - together) * CHUNK, (c + 1) * CHUNK)
-                    nc.vector.quantize_mx(
-                        out=codes[:, pair].bitcast(E4M3),
-                        scales=scales[:, pair],
-                        in_=lay[:, pair, :].rearrange("p n t -> p (n t)"),
-                    )
+                    nc.scalar.activation(out=h_lay[half, b][:, tokens, :], in_=by_token, func=RELU)
+                if c % 2 == 1 and (half == 0 or b == N_BLOCKS - 1):
+                    quantize_h(half, b, c - 1, c + 1)
+
+        def quantize_h(half, b, first, last):
+            tokens = slice(first * CHUNK, last * CHUNK)
+            nc.vector.quantize_mx(
+                out=h_codes[half, b][:, tokens].bitcast(E4M3),
+                scales=h_scales[half, b][:, tokens],
+                in_=h_lay[half, b][:, tokens, :].rearrange("p n t -> p (n t)"),
+            )
 
         banks_o = {}
 
@@ -204,11 +211,10 @@ def tile_list_tabmlp_mix_none_kernel(tc, tab, w1, w8_words, w8_scales, w4_words,
         nc.gpsimd.memset(w4_planes[:], 0)
         load_w_scales(nc.gpsimd, w4_planes, 0, w4_scales)
         lay_out_w1(0, 0, 0, FIRST_COLS, nc.scalar.copy)
-        load_w1(1, 0, SECOND_COLS, "stage0")
+        load_w1(1, 0, BLOCK, "stage0")
         lay_out_w1(0, FIRST_COLS, FIRST_COLS, BLOCK, nc.scalar.copy)
         for quarter in range(4):
             look_up_scales(quarter)
-        load_w1(1, SECOND_COLS, BLOCK, "table_scales")
         load_w1(2, 0, BLOCK, "stage1")
         quantize_w1(0)
         w2 = keep.tile([P, 2 * M + M // 4], I32, name="w2", tag="w_lay0", align_bytes=64)
@@ -221,22 +227,24 @@ def tile_list_tabmlp_mix_none_kernel(tc, tab, w1, w8_words, w8_scales, w4_words,
         nc.sync.dma_start(w4, w4_words.rearrange("a p x -> p a x").bitcast(I32))
         for quarter in range(4):
             look_up_words(quarter)
-        lay_out_w1(1, 0, 0, SECOND_COLS, nc.scalar.copy)
-        lay_out_w1(1, SECOND_COLS, SECOND_COLS, BLOCK, nc.vector.tensor_copy)
+        lay_out_w1(1, 0, 0, BLOCK // 2, nc.vector.tensor_copy)
+        lay_out_w1(1, 0, BLOCK // 2, BLOCK, nc.vector.tensor_copy)
         quantize_w1(1)
-        hidden(0, 0, 4, ())
-        hidden(1, 0, 4, ())
+        hidden(0, 0, range(CHUNKS))
+        hidden(1, 0, range(CHUNKS))
         lay_out_w1(2, 0, 0, BLOCK // 2, nc.vector.tensor_copy)
         lay_out_w1(2, 0, BLOCK // 2, BLOCK, nc.vector.tensor_copy)
         quantize_w1(2)
-        hidden(0, 1, 4, (2,))
-        hidden(1, 1, 4, (2,))
+        hidden(0, 1, range(CHUNKS))
         for n in range(M_TILES):
             project(0, n, 0, 0)
-        hidden(0, 2, 4, (2,))
-        hidden(1, 2, 4, (0, 2))
+        hidden(1, 1, range(CHUNKS))
+        hidden(0, 2, range(CHUNKS))
         for n in range(M_TILES):
             project(0, n, 1, 0)
+        hidden(1, 2, range(CHUNKS))
+        quantize_h(1, 0, 0, CHUNKS)
+        quantize_h(1, 1, 0, CHUNKS)
         for n in range(M_TILES):
             project(0, n, 2, 0)
             emit(0, n)

@@ -44,19 +44,20 @@ def tile_list_tabmlp_mix_none_kernel(tc, tab, w1, w8_words, w8_scales, w4_words,
         tab_scales = keep.tile([P, T // 4], I32, name="tab_scales", align_bytes=64)
         nc.vector.memset(tab_scales[:, 0 : T // 8], 0)
         nc.gpsimd.memset(tab_scales[:, T // 8 : T // 4], 0)
-        warm = keep.tile([P, 1], F32, name="warm", tag="table", align_bytes=64)
-        warm_out = keep.tile([P, 1], F32, name="warm_out", tag="stage1", align_bytes=64)
+        warm = keep.tile([P, 1], F32, name="warm")
+        warm_out = keep.tile([P, 1], F32, name="warm_out")
         nc.vector.memset(warm[:], 0.0)
         nc.scalar.activation(out=warm_out[:], in_=warm[:], func=RELU)
 
-        tab_words = keep.tile([P, T], I32, name="tab_words", tag="table", align_bytes=64)
+        tab_words = keep.tile([P, T], I32, name="tab_words", align_bytes=64)
 
         w1_rows = w1.rearrange("(p j) r -> p j r", j=PACK)
 
         w_raw = {}
 
-        def load_w1(b, first, last, tag):
-            w_raw[b, first] = keep.tile([P, PACK, last - first], F32, name=f"w_raw{b}_{first}", tag=tag, align_bytes=64)
+        def load_w1(b, first, last):
+            name = f"w_raw{b}_{first}"
+            w_raw[b, first] = keep.tile([P, PACK, last - first], F32, name=name, tag=name, align_bytes=64)
             nc.sync.dma_start(w_raw[b, first][:], w1_rows[:, :, b * BLOCK + first : b * BLOCK + last])
 
         def load_w_scales(queue, planes, first_row, source):
@@ -66,12 +67,18 @@ def tile_list_tabmlp_mix_none_kernel(tc, tab, w1, w8_words, w8_scales, w4_words,
                     source[:, 4 * q : 4 * q + 4, :].rearrange("a q n -> q a n").bitcast(I32),
                 )
 
-        load_w1(0, 0, FIRST_COLS, "stage0")
+        load_w1(0, 0, FIRST_COLS)
         scale_rows = tab[0:1, 512 * T : 528 * T].rearrange("o (q t) -> (o q) t", q=16).bitcast(I32)
         for q in range(4):
             nc.sync.dma_start(tab_scales[32 * q + TABLE_ROW : 32 * q + TABLE_ROW + 4, :], scale_rows[4 * q : 4 * q + 4, :])
-        load_w1(0, FIRST_COLS, BLOCK, "stage1")
+        load_w1(0, FIRST_COLS, BLOCK)
         nc.sync.dma_start(tab_words[:], tab[0:1, 0 : 512 * T].rearrange("o (p x) -> (o p) x", p=P).bitcast(I32))
+        load_w1(1, 0, BLOCK)
+        load_w1(2, 0, BLOCK)
+        w8 = keep.tile([P, M], I32, name="w8", align_bytes=64)
+        nc.sync.dma_start(w8[:], w8_words.rearrange("a p n i -> (a p) (n i)").bitcast(I32))
+        w4 = keep.tile([P, 2, M // 2], I32, name="w4", align_bytes=64)
+        nc.sync.dma_start(w4[:], w4_words.rearrange("a p x -> p a x").bitcast(I32))
 
         x_codes = [keep.tile([P, QUARTER], U32, name=f"x_codes{i}", align_bytes=64) for i in range(4)]
         x_scales = [keep.tile([P, QUARTER], U8, name=f"x_scales{i}", align_bytes=64) for i in range(4)]
@@ -93,11 +100,12 @@ def tile_list_tabmlp_mix_none_kernel(tc, tab, w1, w8_words, w8_scales, w4_words,
         w1_scales = [keep.tile([P, BLOCK], U8, name=f"w1_scales{b}", align_bytes=64) for b in range(N_BLOCKS)]
 
         def lay_out_w1(b, loaded_from, first, last, copy):
-            dst = w_lay[b][:].rearrange("p (t m j) -> p m j t", t=PACK, j=PACK)
-            src = w_raw[b, loaded_from][:].rearrange("p j (m t) -> p m j t", t=PACK)
+            u = 1 if b == 0 else 2
+            dst = w_lay[b][:].rearrange("p (u t m j) -> p u m j t", u=u, t=PACK // u, j=PACK)
+            src = w_raw[b, loaded_from][:].rearrange("p j (m u t) -> p u m j t", u=u, t=PACK // u)
             copy(
-                out=dst[:, first // PACK : last // PACK],
-                in_=src[:, (first - loaded_from) // PACK : (last - loaded_from) // PACK],
+                out=dst[:, :, first // PACK : last // PACK],
+                in_=src[:, :, (first - loaded_from) // PACK : (last - loaded_from) // PACK],
             )
 
         def quantize_w1(b):
@@ -117,7 +125,7 @@ def tile_list_tabmlp_mix_none_kernel(tc, tab, w1, w8_words, w8_scales, w4_words,
 
         def hidden(half, b, chunks):
             if (half, b) not in h_lay:
-                lay_tag = "stage0" if half == 1 and b == 0 else f"h_lay{half}{b}"
+                lay_tag = "w_raw1_0" if half == 1 and b == 0 else f"h_lay{half}{b}"
                 codes_tag = "w_lay1" if half == 0 and b == 0 else f"h_codes{half}{b}"
                 h_lay[half, b] = keep.tile([P, HALF, PACK], BF16, name=f"h_lay{half}{b}", tag=lay_tag, align_bytes=64)
                 h_codes[half, b] = keep.tile([P, HALF], U32, name=f"h_codes{half}{b}", tag=codes_tag, align_bytes=64)
@@ -181,50 +189,27 @@ def tile_list_tabmlp_mix_none_kernel(tc, tab, w1, w8_words, w8_scales, w4_words,
 
         def emit(half, n):
             result = store.tile([P, HALF], F32, name="result")
+            if half == 1 and n == M_TILES - 1:
+                for cols in (slice(0, QUARTER), slice(QUARTER, HALF)):
+                    nc.scalar.copy(out=result[:, cols], in_=banks_o[half, n][:, cols])
+                    nc.scalar.dma_start(out[n * P : (n + 1) * P, HALF + cols.start : HALF + cols.stop], result[:, cols])
+                return
             if n % 2 == 1:
                 nc.scalar.copy(out=result[:], in_=banks_o[half, n][:])
             else:
                 nc.vector.tensor_copy(out=result[:], in_=banks_o[half, n][:])
             nc.sync.dma_start(out[n * P : (n + 1) * P, half * HALF : (half + 1) * HALF], result[:])
 
-        def last_tile(quarter, bank_number, copy):
-            n = M_TILES - 1
-            bank = psum.tile([P, QUARTER], F32, name=f"bank{bank_number}")
-            first = quarter * QUARTER
-            passes = [(0, 0, QUARTER)] + [(b, c, c + CHUNK) for b in (1, 2) for c in (0, CHUNK)]
-            for i, (b, lo, hi) in enumerate(passes):
-                lhsT, lhsT_scale = second_weights(n, b)
-                nc.tensor.matmul_mx(
-                    out=bank[:, lo:hi],
-                    lhsT=lhsT,
-                    lhsT_scale=lhsT_scale,
-                    rhs=h_codes[1, b][:, first + lo : first + hi].bitcast(E4M3),
-                    rhs_scale=h_scales[1, b][:, first + lo : first + hi],
-                    start=(i == 0),
-                    stop=(i == len(passes) - 1),
-                )
-            result = store.tile([P, QUARTER], F32, name="result")
-            copy(out=result[:], in_=bank[:])
-            nc.sync.dma_start(out[n * P : (n + 1) * P, HALF + first : HALF + first + QUARTER], result[:])
-
-        w4_planes = keep.tile([P, 2, M // 4], I32, name="w4_planes", align_bytes=64)
-        nc.gpsimd.memset(w4_planes[:], 0)
-        load_w_scales(nc.gpsimd, w4_planes, 0, w4_scales)
+        planes = keep.tile([P, N_BLOCKS, M // 4], I32, name="planes", align_bytes=64)
+        nc.gpsimd.memset(planes[:], 0)
+        w8_plane, w4_planes = planes[:, 0:1, :], planes[:, 1:, :]
+        load_w_scales(nc.gpsimd, w8_plane, W8_ROW, w8_scales)
+        load_w_scales(nc.sync, w4_planes, 0, w4_scales)
         lay_out_w1(0, 0, 0, FIRST_COLS, nc.scalar.copy)
-        load_w1(1, 0, BLOCK, "stage0")
         lay_out_w1(0, FIRST_COLS, FIRST_COLS, BLOCK, nc.scalar.copy)
         for quarter in range(4):
             look_up_scales(quarter)
-        load_w1(2, 0, BLOCK, "stage1")
         quantize_w1(0)
-        w2 = keep.tile([P, 2 * M + M // 4], I32, name="w2", tag="w_lay0", align_bytes=64)
-        w8 = w2[:, 0:M]
-        w4 = w2[:, M : 2 * M].rearrange("p (a x) -> p a x", a=2)
-        w8_plane = w2[:, 2 * M :].rearrange("p (a x) -> p a x", a=1)
-        nc.gpsimd.memset(w2[:, 2 * M :], 0)
-        nc.sync.dma_start(w8, w8_words.rearrange("a p n i -> (a p) (n i)").bitcast(I32))
-        load_w_scales(nc.scalar, w8_plane, W8_ROW, w8_scales)
-        nc.sync.dma_start(w4, w4_words.rearrange("a p x -> p a x").bitcast(I32))
         for quarter in range(4):
             look_up_words(quarter)
         lay_out_w1(1, 0, 0, BLOCK // 2, nc.vector.tensor_copy)
@@ -248,9 +233,7 @@ def tile_list_tabmlp_mix_none_kernel(tc, tab, w1, w8_words, w8_scales, w4_words,
         for n in range(M_TILES):
             project(0, n, 2, 0)
             emit(0, n)
-        for n in range(M_TILES - 1):
+        for n in range(M_TILES):
             for b in range(N_BLOCKS):
                 project(1, n, b, 4)
             emit(1, n)
-        last_tile(0, 7, nc.scalar.copy)
-        last_tile(1, 0, nc.vector.tensor_copy)

@@ -14,6 +14,7 @@ U8 = mybir.dt.uint8
 E4M3 = mybir.dt.float8_e4m3fn_x4
 E2M1 = mybir.dt.float4_e2m1fn_x4
 RELU = mybir.ActivationFunctionType.Relu
+COPY = mybir.ActivationFunctionType.Copy
 
 P = 128
 PACK = 4
@@ -39,15 +40,10 @@ def tile_list_tabmlp_mix_none_kernel(tc, tab, w1, w8_words, w8_scales, w4_words,
         store = ctx.enter_context(tc.tile_pool(name="store", bufs=8))
 
         offsets = keep.tile([P, S // 16], U16, name="offsets")
-        nc.sync.dma_start(offsets[:], offs)
 
         tab_scales = keep.tile([P, T // 4], I32, name="tab_scales", align_bytes=64)
         nc.vector.memset(tab_scales[:, 0 : T // 8], 0)
         nc.gpsimd.memset(tab_scales[:, T // 8 : T // 4], 0)
-        warm = keep.tile([P, 1], F32, name="warm")
-        warm_out = keep.tile([P, 1], F32, name="warm_out")
-        nc.vector.memset(warm[:], 0.0)
-        nc.scalar.activation(out=warm_out[:], in_=warm[:], func=RELU)
 
         tab_words = keep.tile([P, T], I32, name="tab_words", align_bytes=64)
 
@@ -61,16 +57,17 @@ def tile_list_tabmlp_mix_none_kernel(tc, tab, w1, w8_words, w8_scales, w4_words,
             nc.sync.dma_start(w_raw[b, first][:], w1_rows[:, :, b * BLOCK + first : b * BLOCK + last])
 
         def load_w_scales(queue, planes, first_row, source):
-            for q in range(4):
+            for r in range(4):
                 queue.dma_start(
-                    planes[32 * q + first_row : 32 * q + first_row + 4],
-                    source[:, 4 * q : 4 * q + 4, :].rearrange("a q n -> q a n").bitcast(I32),
+                    planes[first_row + r : P : 32],
+                    source[:, r:16:4, :].rearrange("a q n -> q a n").bitcast(I32),
                 )
 
         load_w1(0, 0, FIRST_COLS)
+        nc.sync.dma_start(offsets[:], offs)
         scale_rows = tab[0:1, 512 * T : 528 * T].rearrange("o (q t) -> (o q) t", q=16).bitcast(I32)
-        for q in range(4):
-            nc.sync.dma_start(tab_scales[32 * q + TABLE_ROW : 32 * q + TABLE_ROW + 4, :], scale_rows[4 * q : 4 * q + 4, :])
+        for r in range(4):
+            nc.sync.dma_start(tab_scales[TABLE_ROW + r : P : 32, :], scale_rows[r:16:4, :])
         load_w1(0, FIRST_COLS, BLOCK)
         nc.sync.dma_start(tab_words[:], tab[0:1, 0 : 512 * T].rearrange("o (p x) -> (o p) x", p=P).bitcast(I32))
         load_w1(1, 0, BLOCK)
@@ -107,6 +104,9 @@ def tile_list_tabmlp_mix_none_kernel(tc, tab, w1, w8_words, w8_scales, w4_words,
                 out=dst[:, :, first // PACK : last // PACK],
                 in_=src[:, :, (first - loaded_from) // PACK : (last - loaded_from) // PACK],
             )
+
+        def scalar_copy(out, in_):
+            nc.scalar.activation(out=out, in_=in_, func=COPY)
 
         def quantize_w1(b):
             for i in range(2):
@@ -205,8 +205,8 @@ def tile_list_tabmlp_mix_none_kernel(tc, tab, w1, w8_words, w8_scales, w4_words,
         w8_plane, w4_planes = planes[:, 0:1, :], planes[:, 1:, :]
         load_w_scales(nc.gpsimd, w8_plane, W8_ROW, w8_scales)
         load_w_scales(nc.sync, w4_planes, 0, w4_scales)
-        lay_out_w1(0, 0, 0, FIRST_COLS, nc.scalar.copy)
-        lay_out_w1(0, FIRST_COLS, FIRST_COLS, BLOCK, nc.scalar.copy)
+        lay_out_w1(0, 0, 0, FIRST_COLS, scalar_copy)
+        lay_out_w1(0, FIRST_COLS, FIRST_COLS, BLOCK, scalar_copy)
         for quarter in range(4):
             look_up_scales(quarter)
         quantize_w1(0)

@@ -78,14 +78,12 @@ def tile_list_tabmlp_mix_none_kernel(tc, tab, w1, w8_words, w8_scales, w4_words,
         nc.sync.dma_start(w4[:], w4_words.rearrange("a p x -> p a x").bitcast(I32))
 
         x_codes = [keep.tile([P, QUARTER], U32, name=f"x_codes{i}", align_bytes=64) for i in range(4)]
-        x_scales = [keep.tile([P, QUARTER], U8, name=f"x_scales{i}", align_bytes=64) for i in range(4)]
+        x_scales = keep.tile([P, S], U8, name="x_scales", align_bytes=64)
 
         def look_up(dst, window, quarter):
             part = offsets[:, quarter * QUARTER // 16 : (quarter + 1) * QUARTER // 16]
             nc.vector.tensor_copy(dst[quarter][:], window.indirect(part))
 
-        def look_up_scales(quarter):
-            look_up(x_scales, tab_scales[:].bitcast(U8), quarter)
 
         def look_up_words(quarter):
             look_up(x_codes, tab_words[:].bitcast(U32), quarter)
@@ -109,13 +107,7 @@ def tile_list_tabmlp_mix_none_kernel(tc, tab, w1, w8_words, w8_scales, w4_words,
             nc.scalar.activation(out=out, in_=in_, func=COPY)
 
         def quantize_w1(b):
-            for i in range(2):
-                cols = slice(i * BLOCK // 2, (i + 1) * BLOCK // 2)
-                nc.vector.quantize_mx(
-                    out=w1_codes[b][:, cols].bitcast(E4M3),
-                    scales=w1_scales[b][:, cols],
-                    in_=w_lay[b][:, i * 2 * BLOCK : (i + 1) * 2 * BLOCK],
-                )
+            nc.vector.quantize_mx(out=w1_codes[b][:].bitcast(E4M3), scales=w1_scales[b][:], in_=w_lay[b][:])
 
         h_codes = {}
         h_scales = {}
@@ -144,7 +136,7 @@ def tile_list_tabmlp_mix_none_kernel(tc, tab, w1, w8_words, w8_scales, w4_words,
                         lhsT=w1_codes[b][:, cols].bitcast(E4M3),
                         lhsT_scale=w1_scales[b][:, cols],
                         rhs=x_codes[quarter][:, picked].bitcast(E4M3),
-                        rhs_scale=x_scales[quarter][TABLE_ROW:, picked],
+                        rhs_scale=x_scales[TABLE_ROW:, half * HALF + c * CHUNK : half * HALF + (c + 1) * CHUNK],
                         start=True,
                         stop=True,
                     )
@@ -200,25 +192,23 @@ def tile_list_tabmlp_mix_none_kernel(tc, tab, w1, w8_words, w8_scales, w4_words,
                 nc.vector.tensor_copy(out=result[:], in_=banks_o[half, n][:])
             nc.sync.dma_start(out[n * P : (n + 1) * P, half * HALF : (half + 1) * HALF], result[:])
 
-        planes = keep.tile([P, N_BLOCKS, M // 4], I32, name="planes", align_bytes=64)
-        nc.gpsimd.memset(planes[:], 0)
-        w8_plane, w4_planes = planes[:, 0:1, :], planes[:, 1:, :]
-        load_w_scales(nc.gpsimd, w8_plane, W8_ROW, w8_scales)
+        w4_planes = keep.tile([P, 2, M // 4], I32, name="w4_planes", align_bytes=64)
+        nc.gpsimd.memset(w4_planes[:], 0)
         load_w_scales(nc.sync, w4_planes, 0, w4_scales)
         lay_out_w1(0, 0, 0, FIRST_COLS, scalar_copy)
         lay_out_w1(0, FIRST_COLS, FIRST_COLS, BLOCK, scalar_copy)
-        for quarter in range(4):
-            look_up_scales(quarter)
+        nc.vector.tensor_copy(x_scales[:], tab_scales[:].bitcast(U8).indirect(offsets[:]))
         quantize_w1(0)
+        w8_plane = keep.tile([P, 1, M // 4], I32, name="w8_plane", tag="w_raw0_256", align_bytes=64)
+        nc.gpsimd.memset(w8_plane[:], 0)
+        load_w_scales(nc.scalar, w8_plane, W8_ROW, w8_scales)
         for quarter in range(4):
             look_up_words(quarter)
-        lay_out_w1(1, 0, 0, BLOCK // 2, nc.vector.tensor_copy)
-        lay_out_w1(1, 0, BLOCK // 2, BLOCK, nc.vector.tensor_copy)
+        lay_out_w1(1, 0, 0, BLOCK, nc.vector.tensor_copy)
         quantize_w1(1)
         hidden(0, 0, range(CHUNKS))
         hidden(1, 0, range(CHUNKS))
-        lay_out_w1(2, 0, 0, BLOCK // 2, nc.vector.tensor_copy)
-        lay_out_w1(2, 0, BLOCK // 2, BLOCK, nc.vector.tensor_copy)
+        lay_out_w1(2, 0, 0, BLOCK, nc.vector.tensor_copy)
         quantize_w1(2)
         hidden(0, 1, range(CHUNKS))
         for n in range(M_TILES):

@@ -18,135 +18,96 @@ COPY = mybir.ActivationFunctionType.Copy
 
 P = 128
 PACK = 4
-BLOCK = P * PACK
-N_BLOCKS = H // BLOCK
+GROUP = P * PACK
+GROUPS = H // GROUP
 HALF = 512
 QUARTER = 256
 CHUNK = 128
 CHUNKS = HALF // CHUNK
 M_TILES = M // P
-RING_FIRST, RING = 4, 4
-VECTOR_FROM, VECTOR_EVERY = 6, 4
+SCALE_ROWS = GROUP // 32
+QUADRANT = 32
+QUADRANTS = P // QUADRANT
+
+RING_BANK = M_TILES
+VECTOR_CHUNK = 2
 W8_ROW = 4
 TABLE_ROW = 8
-FIRST_COLS = 256
+FIRST_COLS = GROUP // 2
 
 
-def tile_list_tabmlp_mix_none_kernel(tc, tab, w1, w8_words, w8_scales, w4_words, w4_scales, offs, out):
+def tile_list_tabmlp_mix_none_kernel(
+    tc, tab, w1, w8_words, w8_scales, w4_words, w4_scales, offs, out
+):
     nc = tc.nc
     with ExitStack() as ctx:
         keep = ctx.enter_context(tc.tile_pool(name="keep", bufs=1))
         psum = ctx.enter_context(tc.psum_pool(name="psum", bufs=1))
-        store = ctx.enter_context(tc.tile_pool(name="store", bufs=8))
+        store = ctx.enter_context(tc.tile_pool(name="store", bufs=2 * M_TILES))
 
         offsets = keep.tile([P, S // 16], U16, name="offsets")
 
         tab_scales = keep.tile([P, T // 4], I32, name="tab_scales", align_bytes=64)
-        nc.vector.memset(tab_scales[:, 0 : T // 8], 0)
-        nc.gpsimd.memset(tab_scales[:, T // 8 : T // 4], 0)
+        nc.vector.memset(tab_scales[:], 0)
 
         tab_words = keep.tile([P, T], I32, name="tab_words", align_bytes=64)
 
         w1_rows = w1.rearrange("(p j) r -> p j r", j=PACK)
-
         w_raw = {}
 
         def load_w1(b, first, last):
             name = f"w_raw{b}_{first}"
             w_raw[b, first] = keep.tile([P, PACK, last - first], F32, name=name, tag=name, align_bytes=64)
-            nc.sync.dma_start(w_raw[b, first][:], w1_rows[:, :, b * BLOCK + first : b * BLOCK + last])
+            nc.sync.dma_start(w_raw[b, first][:], w1_rows[:, :, b * GROUP + first : b * GROUP + last])
 
-        def load_w_scales(queue, planes, first_row, source):
-            for r in range(4):
+        def load_planes(queue, planes, first_row, source):
+            for r in range(QUADRANTS):
                 queue.dma_start(
-                    planes[first_row + r : P : 32],
-                    source[:, r:16:4, :].rearrange("a q n -> q a n").bitcast(I32),
+                    planes[first_row + r : P : QUADRANT],
+                    source[:, r:SCALE_ROWS:QUADRANTS, :].rearrange("a q n -> q a n").bitcast(I32),
                 )
 
         load_w1(0, 0, FIRST_COLS)
         nc.sync.dma_start(offsets[:], offs)
-        scale_rows = tab[0:1, 512 * T : 528 * T].rearrange("o (q t) -> (o q) t", q=16).bitcast(I32)
-        for r in range(4):
-            nc.sync.dma_start(tab_scales[TABLE_ROW + r : P : 32, :], scale_rows[r:16:4, :])
-        load_w1(0, FIRST_COLS, BLOCK)
-        nc.sync.dma_start(tab_words[:], tab[0:1, 0 : 512 * T].rearrange("o (p x) -> (o p) x", p=P).bitcast(I32))
-        load_w1(1, 0, BLOCK)
-        load_w1(2, 0, BLOCK)
+        scale_rows = tab[0:1, K * T : (K + SCALE_ROWS) * T].rearrange("o (q t) -> (o q) t", q=SCALE_ROWS).bitcast(I32)
+        for r in range(QUADRANTS):
+            nc.sync.dma_start(tab_scales[TABLE_ROW + r : P : QUADRANT, :], scale_rows[r:SCALE_ROWS:QUADRANTS, :])
+        load_w1(0, FIRST_COLS, GROUP)
+        nc.sync.dma_start(tab_words[:], tab[0:1, 0 : K * T].rearrange("o (p x) -> (o p) x", p=P).bitcast(I32))
+        load_w1(1, 0, GROUP)
+        load_w1(2, 0, GROUP)
         w8 = keep.tile([P, M], I32, name="w8", align_bytes=64)
         nc.sync.dma_start(w8[:], w8_words.rearrange("a p n i -> (a p) (n i)").bitcast(I32))
-        w4 = keep.tile([P, 2, M // 2], I32, name="w4", align_bytes=64)
+        w4 = keep.tile([P, GROUPS - 1, M // 2], I32, name="w4", align_bytes=64)
         nc.sync.dma_start(w4[:], w4_words.rearrange("a p x -> p a x").bitcast(I32))
 
-        x_codes = [keep.tile([P, QUARTER], U32, name=f"x_codes{i}", align_bytes=64) for i in range(4)]
+        x_codes = [keep.tile([P, QUARTER], U32, name=f"x_codes{i}", align_bytes=64) for i in range(S // QUARTER)]
         x_scales = keep.tile([P, S], U8, name="x_scales", align_bytes=64)
 
-        def look_up(dst, window, quarter):
-            part = offsets[:, quarter * QUARTER // 16 : (quarter + 1) * QUARTER // 16]
-            nc.vector.tensor_copy(dst[quarter][:], window.indirect(part))
+        def gather_words(quarter):
+            entries = offsets[:, quarter * QUARTER // 16 : (quarter + 1) * QUARTER // 16]
+            nc.vector.tensor_copy(x_codes[quarter][:], tab_words[:].bitcast(U32).indirect(entries))
 
+        w_lay = [keep.tile([P, PACK * GROUP], BF16, name=f"w_lay{b}", align_bytes=64) for b in range(GROUPS)]
+        w1_codes = [keep.tile([P, GROUP], U32, name=f"w1_codes{b}", align_bytes=64) for b in range(GROUPS)]
+        w1_scales = [keep.tile([P, GROUP], U8, name=f"w1_scales{b}", align_bytes=64) for b in range(GROUPS)]
 
-        def look_up_words(quarter):
-            look_up(x_codes, tab_words[:].bitcast(U32), quarter)
+        def lay_out_on_scalar(first, last):
+            dst = w_lay[0][:].rearrange("p (t m j) -> p m j t", t=PACK, j=PACK)
+            src = w_raw[0, first][:].rearrange("p j (m t) -> p m j t", t=PACK)
+            nc.scalar.activation(out=dst[:, first // PACK : last // PACK], in_=src, func=COPY)
 
-        w_lay = [
-            keep.tile([P, PACK * BLOCK], BF16, name=f"w_lay{b}", tag=f"w_lay{b}", align_bytes=64) for b in range(N_BLOCKS)
-        ]
-        w1_codes = [keep.tile([P, BLOCK], U32, name=f"w1_codes{b}", align_bytes=64) for b in range(N_BLOCKS)]
-        w1_scales = [keep.tile([P, BLOCK], U8, name=f"w1_scales{b}", align_bytes=64) for b in range(N_BLOCKS)]
-
-        def lay_out_w1(b, loaded_from, first, last, copy):
-            u = 1 if b == 0 else 2
-            dst = w_lay[b][:].rearrange("p (u t m j) -> p u m j t", u=u, t=PACK // u, j=PACK)
-            src = w_raw[b, loaded_from][:].rearrange("p j (m u t) -> p u m j t", u=u, t=PACK // u)
-            copy(
-                out=dst[:, :, first // PACK : last // PACK],
-                in_=src[:, :, (first - loaded_from) // PACK : (last - loaded_from) // PACK],
-            )
-
-        def scalar_copy(out, in_):
-            nc.scalar.activation(out=out, in_=in_, func=COPY)
+        def lay_out_on_vector(b):
+            dst = w_lay[b][:].rearrange("p (u e m j) -> p u m j e", u=2, e=2, j=PACK)
+            src = w_raw[b, 0][:].rearrange("p j (m u e) -> p u m j e", u=2, e=2)
+            nc.vector.tensor_copy(out=dst, in_=src)
 
         def quantize_w1(b):
             nc.vector.quantize_mx(out=w1_codes[b][:].bitcast(E4M3), scales=w1_scales[b][:], in_=w_lay[b][:])
 
+        h_lay = {}
         h_codes = {}
         h_scales = {}
-
-        h_lay = {}
-        done = []
-
-        def hidden(half, b, chunks):
-            if (half, b) not in h_lay:
-                lay_tag = "w_raw1_0" if half == 1 and b == 0 else f"h_lay{half}{b}"
-                codes_tag = "w_lay1" if half == 0 and b == 0 else f"h_codes{half}{b}"
-                h_lay[half, b] = keep.tile([P, HALF, PACK], BF16, name=f"h_lay{half}{b}", tag=lay_tag, align_bytes=64)
-                h_codes[half, b] = keep.tile([P, HALF], U32, name=f"h_codes{half}{b}", tag=codes_tag, align_bytes=64)
-                h_scales[half, b] = keep.tile([P, HALF], U8, name=f"h_scales{half}{b}", align_bytes=64)
-            for c in chunks:
-                step = len(done)
-                done.append((half, b, c))
-                tokens = slice(c * CHUNK, (c + 1) * CHUNK)
-                quarter = 2 * half + c // 2
-                picked = slice(c % 2 * CHUNK, (c % 2 + 1) * CHUNK)
-                bank = psum.tile([P, PACK, CHUNK], F32, name=f"bank{RING_FIRST + step % RING}")
-                for t in range(PACK):
-                    cols = slice(t * P, (t + 1) * P)
-                    nc.tensor.matmul_mx(
-                        out=bank[:, t, :],
-                        lhsT=w1_codes[b][:, cols].bitcast(E4M3),
-                        lhsT_scale=w1_scales[b][:, cols],
-                        rhs=x_codes[quarter][:, picked].bitcast(E4M3),
-                        rhs_scale=x_scales[TABLE_ROW:, half * HALF + c * CHUNK : half * HALF + (c + 1) * CHUNK],
-                        start=True,
-                        stop=True,
-                    )
-                by_token = bank[:].rearrange("p t n -> p n t")
-                if step >= VECTOR_FROM and (step - VECTOR_FROM) % VECTOR_EVERY == 0:
-                    nc.vector.tensor_scalar_max(h_lay[half, b][:, tokens, :], by_token, 0.0)
-                else:
-                    nc.scalar.activation(out=h_lay[half, b][:, tokens, :], in_=by_token, func=RELU)
-                if c % 2 == 1 and (half == 0 or b == N_BLOCKS - 1):
-                    quantize_h(half, b, c - 1, c + 1)
 
         def quantize_h(half, b, first, last):
             tokens = slice(first * CHUNK, last * CHUNK)
@@ -156,74 +117,104 @@ def tile_list_tabmlp_mix_none_kernel(tc, tab, w1, w8_words, w8_scales, w4_words,
                 in_=h_lay[half, b][:, tokens, :].rearrange("p n t -> p (n t)"),
             )
 
-        banks_o = {}
+        def hidden(half, b):
+            lay_tag = "w_raw1_0" if (half, b) == (1, 0) else f"h_lay{half}{b}"
+            h_lay[half, b] = keep.tile([P, HALF, PACK], BF16, name=f"h_lay{half}{b}", tag=lay_tag, align_bytes=64)
+            h_codes[half, b] = keep.tile([P, HALF], U32, name=f"h_codes{half}{b}", align_bytes=64)
+            h_scales[half, b] = keep.tile([P, HALF], U8, name=f"h_scales{half}{b}", align_bytes=64)
+            for c in range(CHUNKS):
+                tokens = slice(c * CHUNK, (c + 1) * CHUNK)
+                first = half * HALF + c * CHUNK
+                within = first % QUARTER
+                bank = psum.tile([P, PACK, CHUNK], F32, name=f"bank{RING_BANK + c}")
+                for t in range(PACK):
+                    cols = slice(t * P, (t + 1) * P)
+                    nc.tensor.matmul_mx(
+                        out=bank[:, t, :],
+                        lhsT=w1_codes[b][:, cols].bitcast(E4M3),
+                        lhsT_scale=w1_scales[b][:, cols],
+                        rhs=x_codes[first // QUARTER][:, within : within + CHUNK].bitcast(E4M3),
+                        rhs_scale=x_scales[TABLE_ROW:, first : first + CHUNK],
+                        start=True,
+                        stop=True,
+                    )
+                by_token = bank[:].rearrange("p t n -> p n t")
+                if c == VECTOR_CHUNK and (half, b) != (0, 0):
+                    nc.vector.tensor_scalar_max(h_lay[half, b][:, tokens, :], by_token, 0.0)
+                else:
+                    nc.scalar.activation(out=h_lay[half, b][:, tokens, :], in_=by_token, func=RELU)
+                if c % 2 == 1 and (half == 0 or b == GROUPS - 1):
+                    quantize_h(half, b, c - 1, c + 1)
 
-        def second_weights(n, b):
-            planes = slice(n * P // 4, (n + 1) * P // 4)
-            if b == 0:
-                return w8[:, n * P : (n + 1) * P].bitcast(E4M3), w8_plane[W8_ROW:, 0, planes].bitcast(U8)
-            words = w4[:, b - 1, n * P // 2 : (n + 1) * P // 2]
-            return words.bitcast(U8).bitcast(E2M1), w4_planes[:, b - 1, planes].bitcast(U8)
+        sums = {}
 
-        def project(half, n, b, first_bank):
+        def project(half, n, b):
             if b == 0:
-                banks_o[half, n] = psum.tile([P, HALF], F32, name=f"bank{first_bank + n}")
-            lhsT, lhsT_scale = second_weights(n, b)
+                sums[half, n] = psum.tile([P, HALF], F32, name=f"bank{half * M_TILES + n}")
+            plane_cols = slice(n * P // 4, (n + 1) * P // 4)
+            if b == 0:
+                lhsT = w8[:, n * P : (n + 1) * P].bitcast(E4M3)
+                lhsT_scale = w8_plane[W8_ROW:, 0, plane_cols].bitcast(U8)
+            else:
+                lhsT = w4[:, b - 1, n * P // 2 : (n + 1) * P // 2].bitcast(U8).bitcast(E2M1)
+                lhsT_scale = w4_planes[:, b - 1, plane_cols].bitcast(U8)
             nc.tensor.matmul_mx(
-                out=banks_o[half, n][:],
+                out=sums[half, n][:],
                 lhsT=lhsT,
                 lhsT_scale=lhsT_scale,
                 rhs=h_codes[half, b][:].bitcast(E4M3),
                 rhs_scale=h_scales[half, b][:],
                 start=(b == 0),
-                stop=(b == N_BLOCKS - 1),
+                stop=(b == GROUPS - 1),
             )
 
         def emit(half, n):
             result = store.tile([P, HALF], F32, name="result")
-            if half == 1 and n == M_TILES - 1:
-                for cols in (slice(0, QUARTER), slice(QUARTER, HALF)):
-                    nc.scalar.copy(out=result[:, cols], in_=banks_o[half, n][:, cols])
-                    nc.scalar.dma_start(out[n * P : (n + 1) * P, HALF + cols.start : HALF + cols.stop], result[:, cols])
-                return
-            if n % 2 == 1:
-                nc.scalar.copy(out=result[:], in_=banks_o[half, n][:])
-            else:
-                nc.vector.tensor_copy(out=result[:], in_=banks_o[half, n][:])
-            nc.sync.dma_start(out[n * P : (n + 1) * P, half * HALF : (half + 1) * HALF], result[:])
+            copy = nc.vector.tensor_copy if n % 2 == 0 else nc.scalar.copy
+            parts = 2 if half == 1 and n >= M_TILES - 2 else 1
+            for i in range(parts):
+                cols = slice(i * HALF // parts, (i + 1) * HALF // parts)
+                copy(out=result[:, cols], in_=sums[half, n][:, cols])
+                nc.sync.dma_start(
+                    out[n * P : (n + 1) * P, half * HALF + cols.start : half * HALF + cols.stop], result[:, cols]
+                )
 
-        w4_planes = keep.tile([P, 2, M // 4], I32, name="w4_planes", align_bytes=64)
-        nc.gpsimd.memset(w4_planes[:], 0)
-        load_w_scales(nc.sync, w4_planes, 0, w4_scales)
-        lay_out_w1(0, 0, 0, FIRST_COLS, scalar_copy)
-        lay_out_w1(0, FIRST_COLS, FIRST_COLS, BLOCK, scalar_copy)
+        w4_planes = keep.tile([P, GROUPS - 1, M // 4], I32, name="w4_planes", align_bytes=64)
+        nc.vector.memset(w4_planes[:], 0)
+        load_planes(nc.sync, w4_planes, 0, w4_scales)
+
+        lay_out_on_scalar(0, FIRST_COLS)
+        lay_out_on_scalar(FIRST_COLS, GROUP)
         nc.vector.tensor_copy(x_scales[:], tab_scales[:].bitcast(U8).indirect(offsets[:]))
         quantize_w1(0)
-        w8_plane = keep.tile([P, 1, M // 4], I32, name="w8_plane", tag="w_raw0_256", align_bytes=64)
+
+        w8_plane = keep.tile([P, 1, M // 4], I32, name="w8_plane", tag=f"w_raw0_{FIRST_COLS}", align_bytes=64)
         nc.gpsimd.memset(w8_plane[:], 0)
-        load_w_scales(nc.scalar, w8_plane, W8_ROW, w8_scales)
-        for quarter in range(4):
-            look_up_words(quarter)
-        lay_out_w1(1, 0, 0, BLOCK, nc.vector.tensor_copy)
+        load_planes(nc.scalar, w8_plane, W8_ROW, w8_scales)
+
+        for quarter in range(S // QUARTER):
+            gather_words(quarter)
+        lay_out_on_vector(1)
         quantize_w1(1)
-        hidden(0, 0, range(CHUNKS))
-        hidden(1, 0, range(CHUNKS))
-        lay_out_w1(2, 0, 0, BLOCK, nc.vector.tensor_copy)
+
+        hidden(0, 0)
+        hidden(1, 0)
+        lay_out_on_vector(2)
         quantize_w1(2)
-        hidden(0, 1, range(CHUNKS))
+        hidden(0, 1)
+        hidden(1, 1)
         for n in range(M_TILES):
-            project(0, n, 0, 0)
-        hidden(1, 1, range(CHUNKS))
-        hidden(0, 2, range(CHUNKS))
+            project(0, n, 0)
+        hidden(0, 2)
         for n in range(M_TILES):
-            project(0, n, 1, 0)
-        hidden(1, 2, range(CHUNKS))
+            project(0, n, 1)
+        hidden(1, 2)
         quantize_h(1, 0, 0, CHUNKS)
         quantize_h(1, 1, 0, CHUNKS)
         for n in range(M_TILES):
-            project(0, n, 2, 0)
+            project(0, n, 2)
             emit(0, n)
         for n in range(M_TILES):
-            for b in range(N_BLOCKS):
-                project(1, n, b, 4)
+            for b in range(GROUPS):
+                project(1, n, b)
             emit(1, n)

@@ -33,6 +33,7 @@ RING_BANK = M_TILES
 VECTOR_CHUNK = 2
 W8_ROW = 4
 TABLE_ROW = 8
+ALIGN = 256
 FIRST_COLS = GROUP // 2
 
 
@@ -47,17 +48,17 @@ def tile_list_tabmlp_mix_none_kernel(
 
         offsets = keep.tile([P, S // 16], U16, name="offsets")
 
-        tab_scales = keep.tile([P, T // 4], I32, name="tab_scales", align_bytes=64)
+        tab_scales = keep.tile([P, T // 4], I32, name="tab_scales", align_bytes=ALIGN)
         nc.vector.memset(tab_scales[:], 0)
 
-        tab_words = keep.tile([P, T], I32, name="tab_words", align_bytes=64)
+        tab_words = keep.tile([P, T], I32, name="tab_words", align_bytes=ALIGN)
 
         w1_rows = w1.rearrange("(p j) r -> p j r", j=PACK)
         w_raw = {}
 
         def load_w1(b, first, last):
             name = f"w_raw{b}_{first}"
-            w_raw[b, first] = keep.tile([P, PACK, last - first], F32, name=name, tag=name, align_bytes=64)
+            w_raw[b, first] = keep.tile([P, PACK, last - first], F32, name=name, tag=name, align_bytes=ALIGN)
             nc.sync.dma_start(w_raw[b, first][:], w1_rows[:, :, b * GROUP + first : b * GROUP + last])
 
         def load_planes(queue, planes, first_row, source):
@@ -76,21 +77,21 @@ def tile_list_tabmlp_mix_none_kernel(
         nc.sync.dma_start(tab_words[:], tab[0:1, 0 : K * T].rearrange("o (p x) -> (o p) x", p=P).bitcast(I32))
         load_w1(1, 0, GROUP)
         load_w1(2, 0, GROUP)
-        w8 = keep.tile([P, M], I32, name="w8", align_bytes=64)
+        w8 = keep.tile([P, M], I32, name="w8", align_bytes=ALIGN)
         nc.sync.dma_start(w8[:], w8_words.rearrange("a p n i -> (a p) (n i)").bitcast(I32))
-        w4 = keep.tile([P, GROUPS - 1, M // 2], I32, name="w4", align_bytes=64)
+        w4 = keep.tile([P, GROUPS - 1, M // 2], I32, name="w4", align_bytes=ALIGN)
         nc.sync.dma_start(w4[:], w4_words.rearrange("a p x -> p a x").bitcast(I32))
 
-        x_codes = [keep.tile([P, QUARTER], U32, name=f"x_codes{i}", align_bytes=64) for i in range(S // QUARTER)]
-        x_scales = keep.tile([P, S], U8, name="x_scales", align_bytes=64)
+        x_codes = [keep.tile([P, QUARTER], U32, name=f"x_codes{i}", align_bytes=ALIGN) for i in range(S // QUARTER)]
+        x_scales = keep.tile([P, S], U8, name="x_scales", align_bytes=ALIGN)
 
         def gather_words(quarter):
             entries = offsets[:, quarter * QUARTER // 16 : (quarter + 1) * QUARTER // 16]
             nc.vector.tensor_copy(x_codes[quarter][:], tab_words[:].bitcast(U32).indirect(entries))
 
-        w_lay = [keep.tile([P, PACK * GROUP], BF16, name=f"w_lay{b}", align_bytes=64) for b in range(GROUPS)]
-        w1_codes = [keep.tile([P, GROUP], U32, name=f"w1_codes{b}", align_bytes=64) for b in range(GROUPS)]
-        w1_scales = [keep.tile([P, GROUP], U8, name=f"w1_scales{b}", align_bytes=64) for b in range(GROUPS)]
+        w_lay = [keep.tile([P, PACK * GROUP], BF16, name=f"w_lay{b}", align_bytes=ALIGN) for b in range(GROUPS)]
+        w1_codes = [keep.tile([P, GROUP], U32, name=f"w1_codes{b}", align_bytes=ALIGN) for b in range(GROUPS)]
+        w1_scales = [keep.tile([P, GROUP], U8, name=f"w1_scales{b}", align_bytes=ALIGN) for b in range(GROUPS)]
 
         def lay_out_on_scalar(first, last):
             dst = w_lay[0][:].rearrange("p (t m j) -> p m j t", t=PACK, j=PACK)
@@ -119,9 +120,9 @@ def tile_list_tabmlp_mix_none_kernel(
 
         def hidden(half, b):
             lay_tag = "w_raw1_0" if (half, b) == (1, 0) else f"h_lay{half}{b}"
-            h_lay[half, b] = keep.tile([P, HALF, PACK], BF16, name=f"h_lay{half}{b}", tag=lay_tag, align_bytes=64)
-            h_codes[half, b] = keep.tile([P, HALF], U32, name=f"h_codes{half}{b}", align_bytes=64)
-            h_scales[half, b] = keep.tile([P, HALF], U8, name=f"h_scales{half}{b}", align_bytes=64)
+            h_lay[half, b] = keep.tile([P, HALF, PACK], BF16, name=f"h_lay{half}{b}", tag=lay_tag, align_bytes=ALIGN)
+            h_codes[half, b] = keep.tile([P, HALF], U32, name=f"h_codes{half}{b}", align_bytes=ALIGN)
+            h_scales[half, b] = keep.tile([P, HALF], U8, name=f"h_scales{half}{b}", align_bytes=ALIGN)
             for c in range(CHUNKS):
                 tokens = slice(c * CHUNK, (c + 1) * CHUNK)
                 first = half * HALF + c * CHUNK
@@ -169,7 +170,7 @@ def tile_list_tabmlp_mix_none_kernel(
             )
 
         def emit(half, n):
-            result = store.tile([P, HALF], F32, name="result")
+            result = store.tile([P, HALF], F32, name="result", align_bytes=ALIGN)
             copy = nc.vector.tensor_copy if n % 2 == 0 else nc.scalar.copy
             parts = 2 if half == 1 and n >= M_TILES - 2 else 1
             for i in range(parts):
@@ -179,7 +180,7 @@ def tile_list_tabmlp_mix_none_kernel(
                     out[n * P : (n + 1) * P, half * HALF + cols.start : half * HALF + cols.stop], result[:, cols]
                 )
 
-        w4_planes = keep.tile([P, GROUPS - 1, M // 4], I32, name="w4_planes", align_bytes=64)
+        w4_planes = keep.tile([P, GROUPS - 1, M // 4], I32, name="w4_planes", align_bytes=ALIGN)
         nc.vector.memset(w4_planes[:], 0)
         load_planes(nc.sync, w4_planes, 0, w4_scales)
 
@@ -188,7 +189,7 @@ def tile_list_tabmlp_mix_none_kernel(
         nc.vector.tensor_copy(x_scales[:], tab_scales[:].bitcast(U8).indirect(offsets[:]))
         quantize_w1(0)
 
-        w8_plane = keep.tile([P, 1, M // 4], I32, name="w8_plane", tag=f"w_raw0_{FIRST_COLS}", align_bytes=64)
+        w8_plane = keep.tile([P, 1, M // 4], I32, name="w8_plane", tag=f"w_raw0_{FIRST_COLS}", align_bytes=ALIGN)
         nc.gpsimd.memset(w8_plane[:], 0)
         load_planes(nc.scalar, w8_plane, W8_ROW, w8_scales)
 

@@ -46,7 +46,7 @@ def tile_list_tabmlp_mix_none_kernel(
         psum = ctx.enter_context(tc.psum_pool(name="psum", bufs=1))
         store = ctx.enter_context(tc.tile_pool(name="store", bufs=2 * M_TILES))
 
-        offsets = keep.tile([P, S // 16], U16, name="offsets")
+        offsets = keep.tile([P, S // 16], U16, name="offsets", align_bytes=ALIGN)
 
         tab_scales = keep.tile([P, T // 4], I32, name="tab_scales", align_bytes=ALIGN)
         nc.vector.memset(tab_scales[:], 0)
@@ -89,7 +89,7 @@ def tile_list_tabmlp_mix_none_kernel(
             entries = offsets[:, quarter * QUARTER // 16 : (quarter + 1) * QUARTER // 16]
             nc.vector.tensor_copy(x_codes[quarter][:], tab_words[:].bitcast(U32).indirect(entries))
 
-        w_lay = [keep.tile([P, PACK * GROUP], BF16, name=f"w_lay{b}", align_bytes=ALIGN) for b in range(GROUPS)]
+        w_lay = [keep.tile([P, PACK * GROUP], BF16, name=f"w_lay{b}", tag=f"w_lay{b}", align_bytes=ALIGN) for b in range(GROUPS)]
         w1_codes = [keep.tile([P, GROUP], U32, name=f"w1_codes{b}", align_bytes=ALIGN) for b in range(GROUPS)]
         w1_scales = [keep.tile([P, GROUP], U8, name=f"w1_scales{b}", align_bytes=ALIGN) for b in range(GROUPS)]
 
@@ -189,7 +189,7 @@ def tile_list_tabmlp_mix_none_kernel(
         nc.vector.tensor_copy(x_scales[:], tab_scales[:].bitcast(U8).indirect(offsets[:]))
         quantize_w1(0)
 
-        w8_plane = keep.tile([P, 1, M // 4], I32, name="w8_plane", tag=f"w_raw0_{FIRST_COLS}", align_bytes=ALIGN)
+        w8_plane = keep.tile([P, 1, M // 4], I32, name="w8_plane", tag="w_lay0", align_bytes=ALIGN)
         nc.gpsimd.memset(w8_plane[:], 0)
         load_planes(nc.scalar, w8_plane, W8_ROW, w8_scales)
 

@@ -58,8 +58,9 @@ def tile_list_tabmlp_mix_none_kernel(
 
         def load_w1(b, first, last):
             name = f"w_raw{b}_{first}"
+            start = (b + 1) % GROUPS * GROUP
             w_raw[b, first] = keep.tile([P, PACK, last - first], F32, name=name, tag=name, align_bytes=ALIGN)
-            nc.sync.dma_start(w_raw[b, first][:], w1_rows[:, :, b * GROUP + first : b * GROUP + last])
+            nc.sync.dma_start(w_raw[b, first][:], w1_rows[:, :, start + first : start + last])
 
         def load_planes(queue, planes, first_row, source):
             for r in range(QUADRANTS):
@@ -77,8 +78,6 @@ def tile_list_tabmlp_mix_none_kernel(
         nc.sync.dma_start(tab_words[:], tab[0:1, 0 : K * T].rearrange("o (p x) -> (o p) x", p=P).bitcast(I32))
         load_w1(1, 0, GROUP)
         load_w1(2, 0, GROUP)
-        w8 = keep.tile([P, M], I32, name="w8", align_bytes=ALIGN)
-        nc.sync.dma_start(w8[:], w8_words.rearrange("a p n i -> (a p) (n i)").bitcast(I32))
         w4 = keep.tile([P, GROUPS - 1, M // 2], I32, name="w4", align_bytes=ALIGN)
         nc.sync.dma_start(w4[:], w4_words.rearrange("a p x -> p a x").bitcast(I32))
 
@@ -153,12 +152,12 @@ def tile_list_tabmlp_mix_none_kernel(
             if b == 0:
                 sums[half, n] = psum.tile([P, HALF], F32, name=f"bank{half * M_TILES + n}")
             plane_cols = slice(n * P // 4, (n + 1) * P // 4)
-            if b == 0:
+            if b == GROUPS - 1:
                 lhsT = w8[:, n * P : (n + 1) * P].bitcast(E4M3)
                 lhsT_scale = w8_plane[W8_ROW:, 0, plane_cols].bitcast(U8)
             else:
-                lhsT = w4[:, b - 1, n * P // 2 : (n + 1) * P // 2].bitcast(U8).bitcast(E2M1)
-                lhsT_scale = w4_planes[:, b - 1, plane_cols].bitcast(U8)
+                lhsT = w4[:, b, n * P // 2 : (n + 1) * P // 2].bitcast(U8).bitcast(E2M1)
+                lhsT_scale = w4_planes[:, b, plane_cols].bitcast(U8)
             nc.tensor.matmul_mx(
                 out=sums[half, n][:],
                 lhsT=lhsT,
@@ -180,23 +179,25 @@ def tile_list_tabmlp_mix_none_kernel(
                     out[n * P : (n + 1) * P, half * HALF + cols.start : half * HALF + cols.stop], result[:, cols]
                 )
 
-        w4_planes = keep.tile([P, GROUPS - 1, M // 4], I32, name="w4_planes", align_bytes=ALIGN)
-        nc.vector.memset(w4_planes[:], 0)
-        load_planes(nc.sync, w4_planes, 0, w4_scales)
+        w8_plane = keep.tile([P, 1, M // 4], I32, name="w8_plane", align_bytes=ALIGN)
+        nc.vector.memset(w8_plane[:], 0)
 
         lay_out_on_scalar(0, FIRST_COLS)
         lay_out_on_scalar(FIRST_COLS, GROUP)
         nc.vector.tensor_copy(x_scales[:], tab_scales[:].bitcast(U8).indirect(offsets[:]))
         quantize_w1(0)
 
-        w8_plane = keep.tile([P, 1, M // 4], I32, name="w8_plane", tag="w_lay0", align_bytes=ALIGN)
-        nc.gpsimd.memset(w8_plane[:], 0)
-        load_planes(nc.scalar, w8_plane, W8_ROW, w8_scales)
+        w4_planes = keep.tile([P, GROUPS - 1, M // 4], I32, name="w4_planes", tag="w_lay0", align_bytes=ALIGN)
+        nc.gpsimd.memset(w4_planes[:], 0)
+        load_planes(nc.scalar, w4_planes, 0, w4_scales)
 
         for quarter in range(S // QUARTER):
             gather_words(quarter)
         lay_out_on_vector(1)
         quantize_w1(1)
+        w8 = keep.tile([P, M], I32, name="w8", tag="w_lay1", align_bytes=ALIGN)
+        nc.sync.dma_start(w8[:], w8_words.rearrange("a p n i -> (a p) (n i)").bitcast(I32))
+        load_planes(nc.sync, w8_plane, W8_ROW, w8_scales)
 
         hidden(0, 0)
         hidden(1, 0)

@@ -29,7 +29,9 @@ SCALE_ROWS = GROUP // 32
 QUADRANT = 32
 QUADRANTS = P // QUADRANT
 
-RING_BANK = M_TILES
+BANKS = 8
+RING = 5
+OPEN_SUMS = BANKS - RING
 VECTOR_CHUNK = 2
 W8_ROW = 4
 TABLE_ROW = 8
@@ -44,7 +46,7 @@ def tile_list_tabmlp_mix_none_kernel(
     with ExitStack() as ctx:
         keep = ctx.enter_context(tc.tile_pool(name="keep", bufs=1))
         psum = ctx.enter_context(tc.psum_pool(name="psum", bufs=1))
-        store = ctx.enter_context(tc.tile_pool(name="store", bufs=2 * M_TILES))
+        store = ctx.enter_context(tc.tile_pool(name="store", bufs=2 * M_TILES + 1))
 
         offsets = keep.tile([P, S // 16], U16, name="offsets", align_bytes=ALIGN)
 
@@ -117,6 +119,10 @@ def tile_list_tabmlp_mix_none_kernel(
                 in_=h_lay[half, b][:, tokens, :].rearrange("p n t -> p (n t)"),
             )
 
+        def ring_bank(half, b, c):
+            behind = GROUPS * S // CHUNK - 1 - ((2 * b + half) * CHUNKS + c)
+            return BANKS - 1 - behind % RING
+
         def hidden(half, b):
             lay_tag = "w_raw1_0" if (half, b) == (1, 0) else f"h_lay{half}{b}"
             h_lay[half, b] = keep.tile([P, HALF, PACK], BF16, name=f"h_lay{half}{b}", tag=lay_tag, align_bytes=ALIGN)
@@ -126,7 +132,7 @@ def tile_list_tabmlp_mix_none_kernel(
                 tokens = slice(c * CHUNK, (c + 1) * CHUNK)
                 first = half * HALF + c * CHUNK
                 within = first % QUARTER
-                bank = psum.tile([P, PACK, CHUNK], F32, name=f"bank{RING_BANK + c}")
+                bank = psum.tile([P, PACK, CHUNK], F32, name=f"bank{ring_bank(half, b, c)}")
                 for t in range(PACK):
                     cols = slice(t * P, (t + 1) * P)
                     nc.tensor.matmul_mx(
@@ -148,9 +154,10 @@ def tile_list_tabmlp_mix_none_kernel(
 
         sums = {}
 
-        def project(half, n, b):
+        def project(half, n, b, first=0, last=HALF, bank=None):
             if b == 0:
-                sums[half, n] = psum.tile([P, HALF], F32, name=f"bank{half * M_TILES + n}")
+                bank = half * M_TILES + n if bank is None else bank
+                sums[half, n, first] = psum.tile([P, last - first], F32, name=f"bank{bank}")
             plane_cols = slice(n * P // 4, (n + 1) * P // 4)
             if b == GROUPS - 1:
                 lhsT = w8[:, n * P : (n + 1) * P].bitcast(E4M3)
@@ -159,25 +166,25 @@ def tile_list_tabmlp_mix_none_kernel(
                 lhsT = w4[:, b, n * P // 2 : (n + 1) * P // 2].bitcast(U8).bitcast(E2M1)
                 lhsT_scale = w4_planes[:, b, plane_cols].bitcast(U8)
             nc.tensor.matmul_mx(
-                out=sums[half, n][:],
+                out=sums[half, n, first][:],
                 lhsT=lhsT,
                 lhsT_scale=lhsT_scale,
-                rhs=h_codes[half, b][:].bitcast(E4M3),
-                rhs_scale=h_scales[half, b][:],
+                rhs=h_codes[half, b][:, first:last].bitcast(E4M3),
+                rhs_scale=h_scales[half, b][:, first:last],
                 start=(b == 0),
                 stop=(b == GROUPS - 1),
             )
 
-        def emit(half, n):
-            result = store.tile([P, HALF], F32, name="result", align_bytes=ALIGN)
-            copy = nc.vector.tensor_copy if n % 2 == 0 else nc.scalar.copy
-            parts = 2 if half == 1 and n >= M_TILES - 2 else 1
+        def emit(half, n, copy, first=0, last=HALF, parts=1):
+            result = store.tile([P, last - first], F32, name="result", align_bytes=ALIGN)
+            width = (last - first) // parts
             for i in range(parts):
-                cols = slice(i * HALF // parts, (i + 1) * HALF // parts)
-                copy(out=result[:, cols], in_=sums[half, n][:, cols])
-                nc.sync.dma_start(
-                    out[n * P : (n + 1) * P, half * HALF + cols.start : half * HALF + cols.stop], result[:, cols]
-                )
+                cols = slice(i * width, (i + 1) * width)
+                start = half * HALF + first + cols.start
+                copy(out=result[:, cols], in_=sums[half, n, first][:, cols])
+                nc.sync.dma_start(out[n * P : (n + 1) * P, start : start + width], result[:, cols])
+
+        copies = [nc.vector.tensor_copy, nc.scalar.copy]
 
         w8_plane = keep.tile([P, 1, M // 4], I32, name="w8_plane", align_bytes=ALIGN)
         nc.vector.memset(w8_plane[:], 0)
@@ -195,6 +202,7 @@ def tile_list_tabmlp_mix_none_kernel(
             gather_words(quarter)
         lay_out_on_vector(1)
         quantize_w1(1)
+
         w8 = keep.tile([P, M], I32, name="w8", tag="w_lay1", align_bytes=ALIGN)
         nc.sync.dma_start(w8[:], w8_words.rearrange("a p n i -> (a p) (n i)").bitcast(I32))
         load_planes(nc.sync, w8_plane, W8_ROW, w8_scales)
@@ -205,18 +213,23 @@ def tile_list_tabmlp_mix_none_kernel(
         quantize_w1(2)
         hidden(0, 1)
         hidden(1, 1)
-        for n in range(M_TILES):
+        for n in range(OPEN_SUMS):
             project(0, n, 0)
         hidden(0, 2)
-        for n in range(M_TILES):
+        for n in range(OPEN_SUMS):
             project(0, n, 1)
         hidden(1, 2)
         quantize_h(1, 0, 0, CHUNKS)
         quantize_h(1, 1, 0, CHUNKS)
         for n in range(M_TILES):
-            project(0, n, 2)
-            emit(0, n)
-        for n in range(M_TILES):
+            for b in range(GROUPS - 1 if n < OPEN_SUMS else 0, GROUPS):
+                project(0, n, b)
+            emit(0, n, copies[n % 2])
+        for n in range(M_TILES - 1):
             for b in range(GROUPS):
                 project(1, n, b)
-            emit(1, n)
+            emit(1, n, copies[n % 2], parts=2 if n == M_TILES - 2 else 1)
+        for first, bank, copy in ((0, None, nc.scalar.copy), (QUARTER, 0, nc.vector.tensor_copy)):
+            for b in range(GROUPS):
+                project(1, M_TILES - 1, b, first, first + QUARTER, bank)
+            emit(1, M_TILES - 1, copy, first, first + QUARTER)

@@ -36,6 +36,7 @@ VECTOR_CHUNK = 2
 W8_ROW = 4
 TABLE_ROW = 8
 ALIGN = 256
+LOOK_UPS = (0, 256, 512, 1024)
 FIRST_COLS = GROUP // 2
 
 
@@ -45,12 +46,13 @@ def tile_list_tabmlp_mix_none_kernel(
     nc = tc.nc
     with ExitStack() as ctx:
         keep = ctx.enter_context(tc.tile_pool(name="keep", bufs=1))
+        shared = ctx.enter_context(tc.tile_pool(name="shared", bufs=1))
         psum = ctx.enter_context(tc.psum_pool(name="psum", bufs=1))
         store = ctx.enter_context(tc.tile_pool(name="store", bufs=2 * M_TILES + 1))
 
         offsets = keep.tile([P, S // 16], U16, name="offsets", align_bytes=ALIGN)
 
-        tab_scales = keep.tile([P, T // 4], I32, name="tab_scales", align_bytes=ALIGN)
+        tab_scales = shared.tile([P, T // 4], I32, name="tab_scales", align_bytes=ALIGN, offset=0)
         nc.vector.memset(tab_scales[:], 0)
 
         tab_words = keep.tile([P, T], I32, name="tab_words", align_bytes=ALIGN)
@@ -83,14 +85,15 @@ def tile_list_tabmlp_mix_none_kernel(
         w4 = keep.tile([P, GROUPS - 1, M // 2], I32, name="w4", align_bytes=ALIGN)
         nc.sync.dma_start(w4[:], w4_words.rearrange("a p x -> p a x").bitcast(I32))
 
-        x_codes = [keep.tile([P, QUARTER], U32, name=f"x_codes{i}", align_bytes=ALIGN) for i in range(S // QUARTER)]
+        x_codes = keep.tile([P, S], U32, name="x_codes", align_bytes=ALIGN)
         x_scales = keep.tile([P, S], U8, name="x_scales", align_bytes=ALIGN)
 
-        def gather_words(quarter):
-            entries = offsets[:, quarter * QUARTER // 16 : (quarter + 1) * QUARTER // 16]
-            nc.vector.tensor_copy(x_codes[quarter][:], tab_words[:].bitcast(U32).indirect(entries))
+        def gather_words(first, last):
+            entries = offsets[:, first // 16 : last // 16]
+            nc.vector.tensor_copy(x_codes[:, first:last], tab_words[:].bitcast(U32).indirect(entries))
 
-        w_lay = [keep.tile([P, PACK * GROUP], BF16, name=f"w_lay{b}", tag=f"w_lay{b}", align_bytes=ALIGN) for b in range(GROUPS)]
+        w_lay = [shared.tile([P, PACK * GROUP], BF16, name="w_lay0", align_bytes=ALIGN, offset=T)]
+        w_lay.extend(keep.tile([P, PACK * GROUP], BF16, name=f"w_lay{b}", tag=f"w_lay{b}", align_bytes=ALIGN) for b in range(1, GROUPS))
         w1_codes = [keep.tile([P, GROUP], U32, name=f"w1_codes{b}", align_bytes=ALIGN) for b in range(GROUPS)]
         w1_scales = [keep.tile([P, GROUP], U8, name=f"w1_scales{b}", align_bytes=ALIGN) for b in range(GROUPS)]
 
@@ -131,7 +134,6 @@ def tile_list_tabmlp_mix_none_kernel(
             for c in range(CHUNKS):
                 tokens = slice(c * CHUNK, (c + 1) * CHUNK)
                 first = half * HALF + c * CHUNK
-                within = first % QUARTER
                 bank = psum.tile([P, PACK, CHUNK], F32, name=f"bank{ring_bank(half, b, c)}")
                 for t in range(PACK):
                     cols = slice(t * P, (t + 1) * P)
@@ -139,7 +141,7 @@ def tile_list_tabmlp_mix_none_kernel(
                         out=bank[:, t, :],
                         lhsT=w1_codes[b][:, cols].bitcast(E4M3),
                         lhsT_scale=w1_scales[b][:, cols],
-                        rhs=x_codes[first // QUARTER][:, within : within + CHUNK].bitcast(E4M3),
+                        rhs=x_codes[:, first : first + CHUNK].bitcast(E4M3),
                         rhs_scale=x_scales[TABLE_ROW:, first : first + CHUNK],
                         start=True,
                         stop=True,
@@ -194,12 +196,12 @@ def tile_list_tabmlp_mix_none_kernel(
         nc.vector.tensor_copy(x_scales[:], tab_scales[:].bitcast(U8).indirect(offsets[:]))
         quantize_w1(0)
 
-        w4_planes = keep.tile([P, GROUPS - 1, M // 4], I32, name="w4_planes", tag="w_lay0", align_bytes=ALIGN)
-        nc.gpsimd.memset(w4_planes[:], 0)
+        w4_planes = shared.tile([P, GROUPS, M // 4], I32, name="w4_planes", align_bytes=ALIGN, offset=T - 2 * M)
+        w4_planes = w4_planes[:, : GROUPS - 1]
         load_planes(nc.scalar, w4_planes, 0, w4_scales)
 
-        for quarter in range(S // QUARTER):
-            gather_words(quarter)
+        for first, last in zip(LOOK_UPS, LOOK_UPS[1:]):
+            gather_words(first, last)
         lay_out_on_vector(1)
         quantize_w1(1)
 

@@ -151,8 +151,10 @@ def tile_list_tabmlp_mix_none_kernel(
                     nc.vector.tensor_scalar_max(h_lay[half, b][:, tokens, :], by_token, 0.0)
                 else:
                     nc.scalar.activation(out=h_lay[half, b][:, tokens, :], in_=by_token, func=RELU)
-                if c % 2 == 1 and (half == 0 or b == GROUPS - 1):
+                if c % 2 == 1 and ((half, b) == (0, 0) or b == GROUPS - 1):
                     quantize_h(half, b, c - 1, c + 1)
+            if (half, b) == (0, 1):
+                quantize_h(half, b, 0, CHUNKS)
 
         sums = {}
 
@@ -230,8 +232,8 @@ def tile_list_tabmlp_mix_none_kernel(
         for n in range(M_TILES - 1):
             for b in range(GROUPS):
                 project(1, n, b)
-            emit(1, n, copies[n % 2], parts=2 if n == M_TILES - 2 else 1)
-        for first, bank, copy in ((0, None, nc.scalar.copy), (QUARTER, 0, nc.vector.tensor_copy)):
+            emit(1, n, copies[(n + 1) % 2], parts=2 if n == M_TILES - 2 else 1)
+        for first, bank, copy in ((0, None, nc.vector.tensor_copy), (QUARTER, 0, nc.scalar.copy)):
             for b in range(GROUPS):
                 project(1, M_TILES - 1, b, first, first + QUARTER, bank)
             emit(1, M_TILES - 1, copy, first, first + QUARTER)

@@ -36,6 +36,7 @@ VECTOR_CHUNK = 2
 W8_ROW = 4
 TABLE_ROW = 8
 ALIGN = 256
+NARROW = 16
 LOOK_UPS = (0, 256, 512, 1024)
 FIRST_COLS = GROUP // 2
 
@@ -107,8 +108,20 @@ def tile_list_tabmlp_mix_none_kernel(
             src = w_raw[b, 0][:].rearrange("p j (m u e) -> p u m j e", u=2, e=2)
             nc.vector.tensor_copy(out=dst, in_=src)
 
-        def quantize_w1(b):
-            nc.vector.quantize_mx(out=w1_codes[b][:].bitcast(E4M3), scales=w1_scales[b][:], in_=w_lay[b][:])
+        def lay_out_pair(b, u):
+            dst = w_lay[b][:].rearrange("p (u e m j) -> p u m j e", u=2, e=2, j=PACK)
+            src = w_raw[b, 0][:].rearrange("p j (m u e) -> p u m j e", u=2, e=2)
+            nc.vector.tensor_copy(out=dst[:, u], in_=src[:, u])
+
+        def quantize_w1(b, parts=1):
+            width = GROUP // parts
+            for i in range(parts):
+                cols = slice(i * width, (i + 1) * width)
+                nc.vector.quantize_mx(
+                    out=w1_codes[b][:, cols].bitcast(E4M3),
+                    scales=w1_scales[b][:, cols],
+                    in_=w_lay[b][:, PACK * cols.start : PACK * cols.stop],
+                )
 
         h_lay = {}
         h_codes = {}
@@ -122,9 +135,18 @@ def tile_list_tabmlp_mix_none_kernel(
                 in_=h_lay[half, b][:, tokens, :].rearrange("p n t -> p (n t)"),
             )
 
+        left = GROUPS * S // CHUNK - NARROW
+        early_ring = [OPEN_SUMS] + [BANKS - 1 - (left - 1 - i) % (RING - 1) for i in range(RING - 1)]
+
         def ring_bank(half, b, c):
-            behind = GROUPS * S // CHUNK - 1 - ((2 * b + half) * CHUNKS + c)
-            return BANKS - 1 - behind % RING
+            index = (2 * b + half) * CHUNKS + c
+            if RING <= index < BANKS:
+                return index - RING
+            behind = GROUPS * S // CHUNK - 1 - index
+            if index >= NARROW:
+                return BANKS - 1 - behind % (RING - 1)
+            turn = NARROW - 1 - index - (OPEN_SUMS if index < RING else 0)
+            return early_ring[-1 - turn % RING]
 
         def hidden(half, b):
             lay_tag = "w_raw1_0" if (half, b) == (1, 0) else f"h_lay{half}{b}"
@@ -204,8 +226,9 @@ def tile_list_tabmlp_mix_none_kernel(
 
         for first, last in zip(LOOK_UPS, LOOK_UPS[1:]):
             gather_words(first, last)
-        lay_out_on_vector(1)
-        quantize_w1(1)
+        lay_out_pair(1, 0)
+        lay_out_pair(1, 1)
+        quantize_w1(1, parts=2)
 
         w8 = keep.tile([P, M], I32, name="w8", tag="w_lay1", align_bytes=ALIGN)
         nc.sync.dma_start(w8[:], w8_words.rearrange("a p n i -> (a p) (n i)").bitcast(I32))
@@ -222,12 +245,13 @@ def tile_list_tabmlp_mix_none_kernel(
         hidden(0, 2)
         for n in range(OPEN_SUMS):
             project(0, n, 1)
+        for b in range(GROUPS - 1):
+            project(0, OPEN_SUMS, b)
         hidden(1, 2)
         quantize_h(1, 0, 0, CHUNKS)
         quantize_h(1, 1, 0, CHUNKS)
         for n in range(M_TILES):
-            for b in range(GROUPS - 1 if n < OPEN_SUMS else 0, GROUPS):
-                project(0, n, b)
+            project(0, n, GROUPS - 1)
             emit(0, n, copies[n % 2])
         for n in range(M_TILES - 1):
             for b in range(GROUPS):

@@ -36,7 +36,6 @@ VECTOR_CHUNK = 2
 W8_ROW = 4
 TABLE_ROW = 8
 ALIGN = 256
-NARROW = 16
 LOOK_UPS = (0, 256, 512, 1024)
 FIRST_COLS = GROUP // 2
 
@@ -94,7 +93,8 @@ def tile_list_tabmlp_mix_none_kernel(
             nc.vector.tensor_copy(x_codes[:, first:last], tab_words[:].bitcast(U32).indirect(entries))
 
         w_lay = [shared.tile([P, PACK * GROUP], BF16, name="w_lay0", align_bytes=ALIGN, offset=T)]
-        w_lay.extend(keep.tile([P, PACK * GROUP], BF16, name=f"w_lay{b}", tag=f"w_lay{b}", align_bytes=ALIGN) for b in range(1, GROUPS))
+        for b in range(1, GROUPS):
+            w_lay.append(keep.tile([P, PACK * GROUP], BF16, name=f"w_lay{b}", tag=f"w_lay{b}", align_bytes=ALIGN))
         w1_codes = [keep.tile([P, GROUP], U32, name=f"w1_codes{b}", align_bytes=ALIGN) for b in range(GROUPS)]
         w1_scales = [keep.tile([P, GROUP], U8, name=f"w1_scales{b}", align_bytes=ALIGN) for b in range(GROUPS)]
 
@@ -107,11 +107,6 @@ def tile_list_tabmlp_mix_none_kernel(
             dst = w_lay[b][:].rearrange("p (u e m j) -> p u m j e", u=2, e=2, j=PACK)
             src = w_raw[b, 0][:].rearrange("p j (m u e) -> p u m j e", u=2, e=2)
             nc.vector.tensor_copy(out=dst, in_=src)
-
-        def lay_out_pair(b, u):
-            dst = w_lay[b][:].rearrange("p (u e m j) -> p u m j e", u=2, e=2, j=PACK)
-            src = w_raw[b, 0][:].rearrange("p j (m u e) -> p u m j e", u=2, e=2)
-            nc.vector.tensor_copy(out=dst[:, u], in_=src[:, u])
 
         def quantize_w1(b, parts=1):
             width = GROUP // parts
@@ -135,18 +130,7 @@ def tile_list_tabmlp_mix_none_kernel(
                 in_=h_lay[half, b][:, tokens, :].rearrange("p n t -> p (n t)"),
             )
 
-        left = GROUPS * S // CHUNK - NARROW
-        early_ring = [OPEN_SUMS] + [BANKS - 1 - (left - 1 - i) % (RING - 1) for i in range(RING - 1)]
-
-        def ring_bank(half, b, c):
-            index = (2 * b + half) * CHUNKS + c
-            if RING <= index < BANKS:
-                return index - RING
-            behind = GROUPS * S // CHUNK - 1 - index
-            if index >= NARROW:
-                return BANKS - 1 - behind % (RING - 1)
-            turn = NARROW - 1 - index - (OPEN_SUMS if index < RING else 0)
-            return early_ring[-1 - turn % RING]
+        free = [*range(OPEN_SUMS, BANKS), *range(OPEN_SUMS)]
 
         def hidden(half, b):
             lay_tag = "w_raw1_0" if (half, b) == (1, 0) else f"h_lay{half}{b}"
@@ -156,7 +140,8 @@ def tile_list_tabmlp_mix_none_kernel(
             for c in range(CHUNKS):
                 tokens = slice(c * CHUNK, (c + 1) * CHUNK)
                 first = half * HALF + c * CHUNK
-                bank = psum.tile([P, PACK, CHUNK], F32, name=f"bank{ring_bank(half, b, c)}")
+                number = free.pop(0)
+                bank = psum.tile([P, PACK, CHUNK], F32, name=f"bank{number}")
                 for t in range(PACK):
                     cols = slice(t * P, (t + 1) * P)
                     nc.tensor.matmul_mx(
@@ -173,6 +158,8 @@ def tile_list_tabmlp_mix_none_kernel(
                     nc.vector.tensor_scalar_max(h_lay[half, b][:, tokens, :], by_token, 0.0)
                 else:
                     nc.scalar.activation(out=h_lay[half, b][:, tokens, :], in_=by_token, func=RELU)
+                if number >= OPEN_SUMS:
+                    free.append(number)
                 if c % 2 == 1 and ((half, b) == (0, 0) or b == GROUPS - 1):
                     quantize_h(half, b, c - 1, c + 1)
             if (half, b) == (0, 1):
@@ -180,10 +167,9 @@ def tile_list_tabmlp_mix_none_kernel(
 
         sums = {}
 
-        def project(half, n, b, first=0, last=HALF, bank=None):
+        def project(half, n, b, number=None, first=0, last=HALF):
             if b == 0:
-                bank = half * M_TILES + n if bank is None else bank
-                sums[half, n, first] = psum.tile([P, last - first], F32, name=f"bank{bank}")
+                sums[half, n, first] = psum.tile([P, last - first], F32, name=f"bank{number}")
             plane_cols = slice(n * P // 4, (n + 1) * P // 4)
             if b == GROUPS - 1:
                 lhsT = w8[:, n * P : (n + 1) * P].bitcast(E4M3)
@@ -220,14 +206,13 @@ def tile_list_tabmlp_mix_none_kernel(
         nc.vector.tensor_copy(x_scales[:], tab_scales[:].bitcast(U8).indirect(offsets[:]))
         quantize_w1(0)
 
-        w4_planes = shared.tile([P, GROUPS, M // 4], I32, name="w4_planes", align_bytes=ALIGN, offset=T - 2 * M)
-        w4_planes = w4_planes[:, : GROUPS - 1]
+        w4_tile = shared.tile([P, GROUPS, M // 4], I32, name="w4_planes", align_bytes=ALIGN, offset=T - 2 * M)
+        w4_planes = w4_tile[:, : GROUPS - 1]
         load_planes(nc.scalar, w4_planes, 0, w4_scales)
 
         for first, last in zip(LOOK_UPS, LOOK_UPS[1:]):
             gather_words(first, last)
-        lay_out_pair(1, 0)
-        lay_out_pair(1, 1)
+        lay_out_on_vector(1)
         quantize_w1(1, parts=2)
 
         w8 = keep.tile([P, M], I32, name="w8", tag="w_lay1", align_bytes=ALIGN)
@@ -241,12 +226,13 @@ def tile_list_tabmlp_mix_none_kernel(
         hidden(0, 1)
         hidden(1, 1)
         for n in range(OPEN_SUMS):
-            project(0, n, 0)
+            project(0, n, 0, n)
+        fourth_bank = free.pop(0)
         hidden(0, 2)
         for n in range(OPEN_SUMS):
             project(0, n, 1)
         for b in range(GROUPS - 1):
-            project(0, OPEN_SUMS, b)
+            project(0, OPEN_SUMS, b, fourth_bank)
         hidden(1, 2)
         quantize_h(1, 0, 0, CHUNKS)
         quantize_h(1, 1, 0, CHUNKS)
@@ -254,10 +240,11 @@ def tile_list_tabmlp_mix_none_kernel(
             project(0, n, GROUPS - 1)
             emit(0, n, copies[n % 2])
         for n in range(M_TILES - 1):
+            number = free.pop(0)
             for b in range(GROUPS):
-                project(1, n, b)
+                project(1, n, b, number)
             emit(1, n, copies[(n + 1) % 2], parts=2 if n == M_TILES - 2 else 1)
-        for first, bank, copy in ((0, None, nc.vector.tensor_copy), (QUARTER, 0, nc.scalar.copy)):
+        for first, number, copy in zip((0, QUARTER), (free.pop(0), 0), copies):
             for b in range(GROUPS):
-                project(1, M_TILES - 1, b, first, first + QUARTER, bank)
+                project(1, M_TILES - 1, b, number, first, first + QUARTER)
             emit(1, M_TILES - 1, copy, first, first + QUARTER)

from contextlib import ExitStack

import concourse.mybir as mybir

K, H, M, T, S = 512, 1536, 512, 2048, 1024
FLOPS = 2 * S * (K * H + H * M)

F32 = mybir.dt.float32
BF16 = mybir.dt.bfloat16
I32 = mybir.dt.int32
U32 = mybir.dt.uint32
U16 = mybir.dt.uint16
U8 = mybir.dt.uint8
E4M3 = mybir.dt.float8_e4m3fn_x4
E2M1 = mybir.dt.float4_e2m1fn_x4
RELU = mybir.ActivationFunctionType.Relu
COPY = mybir.ActivationFunctionType.Copy

P = 128
PACK = 4
GROUP = P * PACK
GROUPS = H // GROUP
HALF = 512
QUARTER = 256
CHUNK = 128
CHUNKS = HALF // CHUNK
M_TILES = M // P
SCALE_ROWS = GROUP // 32
QUADRANT = 32
QUADRANTS = P // QUADRANT

BANKS = 8
RING = 5
OPEN_SUMS = BANKS - RING
VECTOR_CHUNK = 2
W8_ROW = 4
TABLE_ROW = 8
ALIGN = 256
LOOK_UPS = (0, 256, 512, 1024)
FIRST_COLS = GROUP // 2


def tile_list_tabmlp_mix_none_kernel(
    tc, tab, w1, w8_words, w8_scales, w4_words, w4_scales, offs, out
):
    nc = tc.nc
    with ExitStack() as ctx:
        keep = ctx.enter_context(tc.tile_pool(name="keep", bufs=1))
        shared = ctx.enter_context(tc.tile_pool(name="shared", bufs=1))
        psum = ctx.enter_context(tc.psum_pool(name="psum", bufs=1))
        store = ctx.enter_context(tc.tile_pool(name="store", bufs=2 * M_TILES + 1))

        offsets = keep.tile([P, S // 16], U16, name="offsets", align_bytes=ALIGN)

        tab_scales = shared.tile([P, T // 4], I32, name="tab_scales", align_bytes=ALIGN, offset=0)
        nc.vector.memset(tab_scales[:], 0)

        tab_words = keep.tile([P, T], I32, name="tab_words", align_bytes=ALIGN)

        w1_rows = w1.rearrange("(p j) r -> p j r", j=PACK)
        w_raw = {}

        def load_w1(b, first, last):
            name = f"w_raw{b}_{first}"
            start = (b + 1) % GROUPS * GROUP
            w_raw[b, first] = keep.tile([P, PACK, last - first], F32, name=name, tag=name, align_bytes=ALIGN)
            nc.sync.dma_start(w_raw[b, first][:], w1_rows[:, :, start + first : start + last])

        def load_planes(queue, planes, first_row, source):
            for r in range(QUADRANTS):
                queue.dma_start(
                    planes[first_row + r : P : QUADRANT],
                    source[:, r:SCALE_ROWS:QUADRANTS, :].rearrange("a q n -> q a n").bitcast(I32),
                )

        load_w1(0, 0, FIRST_COLS)
        nc.sync.dma_start(offsets[:], offs)
        scale_rows = tab[0:1, K * T : (K + SCALE_ROWS) * T].rearrange("o (q t) -> (o q) t", q=SCALE_ROWS).bitcast(I32)
        for r in range(QUADRANTS):
            nc.sync.dma_start(tab_scales[TABLE_ROW + r : P : QUADRANT, :], scale_rows[r:SCALE_ROWS:QUADRANTS, :])
        load_w1(0, FIRST_COLS, GROUP)
        nc.sync.dma_start(tab_words[:], tab[0:1, 0 : K * T].rearrange("o (p x) -> (o p) x", p=P).bitcast(I32))
        load_w1(1, 0, GROUP)
        load_w1(2, 0, GROUP)
        w4 = keep.tile([P, GROUPS - 1, M // 2], I32, name="w4", align_bytes=ALIGN)
        nc.sync.dma_start(w4[:], w4_words.rearrange("a p x -> p a x").bitcast(I32))

        x_codes = keep.tile([P, S], U32, name="x_codes", align_bytes=ALIGN)
        x_scales = keep.tile([P, S], U8, name="x_scales", align_bytes=ALIGN)

        def gather_words(first, last):
            entries = offsets[:, first // 16 : last // 16]
            nc.vector.tensor_copy(x_codes[:, first:last], tab_words[:].bitcast(U32).indirect(entries))

        w_lay = [shared.tile([P, PACK * GROUP], BF16, name="w_lay0", align_bytes=ALIGN, offset=T)]
        for b in range(1, GROUPS):
            w_lay.append(keep.tile([P, PACK * GROUP], BF16, name=f"w_lay{b}", tag=f"w_lay{b}", align_bytes=ALIGN))
        w1_codes = [keep.tile([P, GROUP], U32, name=f"w1_codes{b}", align_bytes=ALIGN) for b in range(GROUPS)]
        w1_scales = [keep.tile([P, GROUP], U8, name=f"w1_scales{b}", align_bytes=ALIGN) for b in range(GROUPS)]

        def lay_out_on_scalar(first, last):
            dst = w_lay[0][:].rearrange("p (t m j) -> p m j t", t=PACK, j=PACK)
            src = w_raw[0, first][:].rearrange("p j (m t) -> p m j t", t=PACK)
            nc.scalar.activation(out=dst[:, first // PACK : last // PACK], in_=src, func=COPY)

        def lay_out_on_vector(b):
            dst = w_lay[b][:].rearrange("p (u e m j) -> p u m j e", u=2, e=2, j=PACK)
            src = w_raw[b, 0][:].rearrange("p j (m u e) -> p u m j e", u=2, e=2)
            nc.vector.tensor_copy(out=dst, in_=src)

        def quantize_w1(b, parts=1):
            width = GROUP // parts
            for i in range(parts):
                cols = slice(i * width, (i + 1) * width)
                nc.vector.quantize_mx(
                    out=w1_codes[b][:, cols].bitcast(E4M3),
                    scales=w1_scales[b][:, cols],
                    in_=w_lay[b][:, PACK * cols.start : PACK * cols.stop],
                )

        h_lay = {}
        h_codes = {}
        h_scales = {}

        def quantize_h(half, b, first, last):
            tokens = slice(first * CHUNK, last * CHUNK)
            nc.vector.quantize_mx(
                out=h_codes[half, b][:, tokens].bitcast(E4M3),
                scales=h_scales[half, b][:, tokens],
                in_=h_lay[half, b][:, tokens, :].rearrange("p n t -> p (n t)"),
            )

        free = [*range(OPEN_SUMS, BANKS), *range(OPEN_SUMS)]

        def hidden(half, b):
            lay_tag = "w_raw1_0" if (half, b) == (1, 0) else f"h_lay{half}{b}"
            h_lay[half, b] = keep.tile([P, HALF, PACK], BF16, name=f"h_lay{half}{b}", tag=lay_tag, align_bytes=ALIGN)
            h_codes[half, b] = keep.tile([P, HALF], U32, name=f"h_codes{half}{b}", align_bytes=ALIGN)
            h_scales[half, b] = keep.tile([P, HALF], U8, name=f"h_scales{half}{b}", align_bytes=ALIGN)
            for c in range(CHUNKS):
                tokens = slice(c * CHUNK, (c + 1) * CHUNK)
                first = half * HALF + c * CHUNK
                number = free.pop(0)
                bank = psum.tile([P, PACK, CHUNK], F32, name=f"bank{number}")
                for t in range(PACK):
                    cols = slice(t * P, (t + 1) * P)
                    nc.tensor.matmul_mx(
                        out=bank[:, t, :],
                        lhsT=w1_codes[b][:, cols].bitcast(E4M3),
                        lhsT_scale=w1_scales[b][:, cols],
                        rhs=x_codes[:, first : first + CHUNK].bitcast(E4M3),
                        rhs_scale=x_scales[TABLE_ROW:, first : first + CHUNK],
                        start=True,
                        stop=True,
                    )
                by_token = bank[:].rearrange("p t n -> p n t")
                if c == VECTOR_CHUNK and (half, b) != (0, 0):
                    nc.vector.tensor_scalar_max(h_lay[half, b][:, tokens, :], by_token, 0.0)
                else:
                    nc.scalar.activation(out=h_lay[half, b][:, tokens, :], in_=by_token, func=RELU)
                if number >= OPEN_SUMS:
                    free.append(number)
                if c % 2 == 1 and ((half, b) == (0, 0) or b == GROUPS - 1):
                    quantize_h(half, b, c - 1, c + 1)
            if (half, b) == (0, 1):
                quantize_h(half, b, 0, CHUNKS)

        sums = {}

        def project(half, n, b, number=None, first=0, last=HALF):
            if b == 0:
                sums[half, n, first] = psum.tile([P, last - first], F32, name=f"bank{number}")
            plane_cols = slice(n * P // 4, (n + 1) * P // 4)
            if b == GROUPS - 1:
                lhsT = w8[:, n * P : (n + 1) * P].bitcast(E4M3)
                lhsT_scale = w8_plane[W8_ROW:, 0, plane_cols].bitcast(U8)
            else:
                lhsT = w4[:, b, n * P // 2 : (n + 1) * P // 2].bitcast(U8).bitcast(E2M1)
                lhsT_scale = w4_planes[:, b, plane_cols].bitcast(U8)
            nc.tensor.matmul_mx(
                out=sums[half, n, first][:],
                lhsT=lhsT,
                lhsT_scale=lhsT_scale,
                rhs=h_codes[half, b][:, first:last].bitcast(E4M3),
                rhs_scale=h_scales[half, b][:, first:last],
                start=(b == 0),
                stop=(b == GROUPS - 1),
            )

        def emit(half, n, copy, first=0, last=HALF, parts=1):
            result = store.tile([P, last - first], F32, name="result", align_bytes=ALIGN)
            width = (last - first) // parts
            for i in range(parts):
                cols = slice(i * width, (i + 1) * width)
                start = half * HALF + first + cols.start
                copy(out=result[:, cols], in_=sums[half, n, first][:, cols])
                nc.sync.dma_start(out[n * P : (n + 1) * P, start : start + width], result[:, cols])

        copies = [nc.vector.tensor_copy, nc.scalar.copy]

        w8_plane = keep.tile([P, 1, M // 4], I32, name="w8_plane", align_bytes=ALIGN)
        nc.vector.memset(w8_plane[:], 0)

        lay_out_on_scalar(0, FIRST_COLS)
        lay_out_on_scalar(FIRST_COLS, GROUP)
        nc.vector.tensor_copy(x_scales[:], tab_scales[:].bitcast(U8).indirect(offsets[:]))
        quantize_w1(0)

        w4_tile = shared.tile([P, GROUPS, M // 4], I32, name="w4_planes", align_bytes=ALIGN, offset=T - 2 * M)
        w4_planes = w4_tile[:, : GROUPS - 1]
        load_planes(nc.scalar, w4_planes, 0, w4_scales)

        for first, last in zip(LOOK_UPS, LOOK_UPS[1:]):
            gather_words(first, last)
        lay_out_on_vector(1)
        quantize_w1(1, parts=2)

        w8 = keep.tile([P, M], I32, name="w8", tag="w_lay1", align_bytes=ALIGN)
        nc.sync.dma_start(w8[:], w8_words.rearrange("a p n i -> (a p) (n i)").bitcast(I32))
        load_planes(nc.sync, w8_plane, W8_ROW, w8_scales)

        hidden(0, 0)
        hidden(1, 0)
        lay_out_on_vector(2)
        quantize_w1(2)
        hidden(0, 1)
        hidden(1, 1)
        for n in range(OPEN_SUMS):
            project(0, n, 0, n)
        fourth_bank = free.pop(0)
        hidden(0, 2)
        for n in range(OPEN_SUMS):
            project(0, n, 1)
        for b in range(GROUPS - 1):
            project(0, OPEN_SUMS, b, fourth_bank)
        hidden(1, 2)
        quantize_h(1, 0, 0, CHUNKS)
        quantize_h(1, 1, 0, CHUNKS)
        for n in range(M_TILES):
            project(0, n, GROUPS - 1)
            emit(0, n, copies[n % 2])
        for n in range(M_TILES - 1):
            number = free.pop(0)
            for b in range(GROUPS):
                project(1, n, b, number)
            emit(1, n, copies[(n + 1) % 2], parts=2 if n == M_TILES - 2 else 1)
        for first, number, copy in zip((0, QUARTER), (free.pop(0), 0), copies):
            for b in range(GROUPS):
                project(1, M_TILES - 1, b, number, first, first + QUARTER)
            emit(1, M_TILES - 1, copy, first, first + QUARTER)
